import numpy as np
import ml_dtypes


def mxq(x, axis, fmt="e4m3"):
    dtype, down = {"e4m3": (ml_dtypes.float8_e4m3fn, 7), "e5m2": (ml_dtypes.float8_e5m2, 14)}[fmt]
    v = np.moveaxis(np.asarray(x, np.float32).astype(ml_dtypes.bfloat16).astype(np.float64), axis, -1)
    blocks = v.reshape(v.shape[:-1] + (-1, 32))
    amax = np.abs(blocks).max(-1, keepdims=True)
    byte = np.maximum(np.where(amax > 0, np.frexp(amax)[1] - 1 + 127, 0) - down, 1)
    scale = np.exp2(byte - 127.0)
    codes = (blocks / scale).astype(np.float32).astype(dtype).astype(np.float64)
    return np.moveaxis((codes * scale).reshape(v.shape), -1, axis)


WIDE = False


def mx_kscale(k):
    if not WIDE:
        return np.ones(k)
    levels = np.array([24, -24, 12, -12, 0])
    if k % 512:
        return np.exp2(np.random.permutation(np.resize(levels, k // 32))).repeat(32)
    a = np.empty((k // 512, 16))
    for p in range(k // 512):
        a[p, :8] = np.random.permutation(np.resize(levels, 8))
        for g in range(8):
            far = levels[np.abs(levels - a[p, g]) >= 10]
            a[p, g + 8] = far[np.random.randint(len(far))]
    return np.exp2(a.ravel()).repeat(32)


def f64(x):
    return np.asarray(x).astype(np.float64)


def striped(idx):
    return np.tile(idx.reshape(-1, 16).T, (8, 1)).astype(np.uint16)


def unstriped(offs):
    return offs[:16].T.reshape(-1).astype(np.int64)


E2M1 = np.array([0.0, 0.5, 1.0, 1.5, 2.0, 3.0, 4.0, 6.0, -0.0, -0.5, -1.0, -1.5, -2.0, -3.0, -4.0, -6.0])


def pack_weight(w, fmt):
    k, n = w.shape
    w = f64(np.asarray(w, np.float32).astype(ml_dtypes.bfloat16)).reshape(k // 32, 32, n)
    amax = np.abs(w).max(1)
    if fmt == "e4m3":
        byte = np.frexp(amax)[1] - 1 + 127 - 7
    else:
        mant, ex = np.frexp(amax / 6.0)
        byte = np.where(mant > 0.5, ex, ex - 1) + 127
    byte = np.clip(np.where(amax > 0, byte, 1), 1, 254)
    scaled = (w * np.exp2(127.0 - byte)[:, None, :]).reshape(k, n).astype(np.float32)
    by_word = np.ascontiguousarray(scaled.reshape(k // 512, 128, 4, n).transpose(0, 1, 3, 2))
    if fmt == "e4m3":
        words = by_word.astype(ml_dtypes.float8_e4m3fn).view(np.uint8)
    else:
        c = by_word.astype(ml_dtypes.float4_e2m1fn).view(np.uint8) & 0xF
        words = (c[..., 0::2] | (c[..., 1::2] << 4)).reshape(k // 512, 128, 2 * n)
    return np.ascontiguousarray(words), np.ascontiguousarray(byte.astype(np.uint8).reshape(k // 512, 16, n))


def unpack_weight(words, scales, fmt):
    g, _, n = scales.shape
    words = np.ascontiguousarray(words).reshape(g, 128, n, -1)
    if fmt == "e4m3":
        vals = words.view(ml_dtypes.float8_e4m3fn).astype(np.float64)
    else:
        nib = np.empty((g, 128, n, 4), np.uint8)
        nib[..., 0::2] = words & 0xF
        nib[..., 1::2] = words >> 4
        vals = E2M1[nib]
    vals = vals * np.repeat(np.exp2(scales.astype(np.float64) - 127.0), 8, axis=1)[..., None]
    return vals.transpose(0, 1, 3, 2).reshape(g * 512, n)


def pack_table4(v):
    words, scales = pack_weight(v, "e2m1")
    g, t = words.shape[0] // 2, v.shape[1]
    return np.ascontiguousarray(words.reshape(g, 2, 128, t, 2).transpose(0, 2, 3, 1, 4).reshape(g, 128, t, 4)), scales


def unpack_table4(words, scales):
    g, _, t, _ = words.shape
    return unpack_weight(words.reshape(g, 128, t, 2, 2).transpose(0, 3, 1, 2, 4).reshape(2 * g, 128, 2 * t), scales, "e2m1")


def silu(f):
    return f / (1.0 + np.exp(-np.maximum(f, -700.0)))


def sigm(f):
    return 1.0 / (1.0 + np.exp(-np.maximum(f, -700.0)))


K, N, T, J = 1024, 512, 2048, 1024


def setup_inputs():
    n = np.random.standard_normal
    s = mx_kscale(K)[:, None]
    wg = n((K, N)) / np.sqrt(K) / s
    p_tab = pack_table4(n((K, T)) * s)
    p_wg8 = pack_weight(wg[:512], "e4m3")
    p_wg4 = pack_weight(wg[512:], "e2m1")
    return {
        "tab_words": p_tab[0],
        "tab_scales": p_tab[1],
        "wg8_words": p_wg8[0],
        "wg8_scales": p_wg8[1],
        "wg4_words": p_wg4[0],
        "wg4_scales": p_wg4[1],
        "wh": (n((K, N)) / np.sqrt(K) / s).astype(np.float32),
        "bg": (0.3 * n(N) - 1.0).astype(np.float32),
        "rT": (n((N, T))).astype(np.float32),
        "offs": striped(np.random.permutation(T)[:J]),
    }


def reference(tab_words, tab_scales, wg8_words, wg8_scales, wg4_words, wg4_scales, wh, bg, rT, offs):
    idx = unstriped(offs)
    tab_ = unpack_table4(tab_words, tab_scales)[:, idx]
    wg8_ = unpack_weight(wg8_words, wg8_scales, "e4m3")
    wg4_ = unpack_weight(wg4_words, wg4_scales, "e2m1")
    wh_ = mxq(f64(wh), 0, "e4m3")
    ga = wg8_.T @ tab_[:512] + wg4_.T @ tab_[512:]
    gate = sigm(ga + f64(bg)[:, None])
    ha = wh_.T @ tab_
    return f64(rT)[:, idx] + gate * (silu(ha) - f64(rT)[:, idx])

@@ -1,0 +1,219 @@
+from contextlib import ExitStack
+
+import concourse.mybir as mybir
+
+K, N, T, J = 1024, 512, 2048, 1024
+FLOPS = 2 * 2 * K * N * J
+
+F32 = mybir.dt.float32
+BF16 = mybir.dt.bfloat16
+I32 = mybir.dt.int32
+U32 = mybir.dt.uint32
+U16 = mybir.dt.uint16
+U8 = mybir.dt.uint8
+FP8X4 = mybir.dt.float8_e4m3fn_x4
+FP4X4 = mybir.dt.float4_e2m1fn_x4
+ACT = mybir.ActivationFunctionType
+ALU = mybir.AluOpType
+
+P = 128
+PACK = 4
+PASSES = 2
+CHUNKS = N // P
+HALF = 512
+HALVES = J // HALF
+GROUP = 16
+LIVE = 24
+
+
+def tile_list_hwayt_mix_silu_kernel(
+    tc, tab_words, tab_scales, wg8_words, wg8_scales, wg4_words, wg4_scales, wh, bg, rT, offs, out
+):
+    nc = tc.nc
+    with ExitStack() as ctx:
+        keep = ctx.enter_context(tc.tile_pool(name="keep", bufs=1))
+        ring = ctx.enter_context(tc.tile_pool(name="ring", bufs=3))
+        stream = ctx.enter_context(tc.tile_pool(name="stream", bufs=4))
+        psum = ctx.enter_context(tc.psum_pool(name="psum", bufs=1))
+
+        offsets = keep.tile([P, J // GROUP], U16, name="offsets")
+        scale_window = keep.tile([P, T // 4], I32, name="scale_window", align_bytes=64)
+        picked_scales = keep.tile([P, J], U8, name="picked_scales", align_bytes=64)
+        shifted_scales = keep.tile([P, PASSES, J // 4], I32, name="shifted_scales", align_bytes=64)
+        wg8_codes = keep.tile([P, N], I32, name="wg8_codes", align_bytes=64)
+        wg4_codes = keep.tile([P, N // 2], I32, name="wg4_codes", align_bytes=64)
+        wg8_plane = keep.tile([P, N // 4], I32, name="wg8_plane", align_bytes=64)
+        wg4_plane = keep.tile([P, N // 4], I32, name="wg4_plane", align_bytes=64)
+        wh_first = keep.tile([P, PASSES, PACK, P], F32, name="wh_first")
+        bias = keep.tile([P, CHUNKS], F32, name="bias")
+        neg_bias = keep.tile([P, CHUNKS], F32, name="neg_bias")
+        warm_in = keep.tile([P, 1], F32, name="warm_in")
+        warm_out = keep.tile([P, 1], F32, name="warm_out")
+
+        for q in range(4):
+            nc.vector.memset(scale_window[32 * q : 32 * q + LIVE, :], 0)
+        nc.vector.memset(warm_in[:], 0.0)
+        nc.vector.memset(shifted_scales[96:P], 0)
+        nc.scalar.activation(warm_out[:], warm_in[:], ACT.Sigmoid)
+
+        def load_plane(plane, scales, q):
+            rows = scales[0].bitcast(I32)[4 * q : 4 * q + 4, :]
+            nc.sync.dma_start(plane[32 * q : 32 * (q + 1), :], rows.unsqueeze(0).to_broadcast([8, 4, N // 4]))
+
+        wh_rows = wh.rearrange("(a p i) n -> a p i n", a=PASSES, i=PACK)
+        nc.sync.dma_start(offsets[:], offs)
+        for q in range(4):
+            nc.sync.dma_start(
+                scale_window[32 * q + LIVE : 32 * (q + 1), :], tab_scales.bitcast(I32)[:, 4 * q : 4 * q + 4, :]
+            )
+        word_window = stream.tile([P, T], I32, name="word_window", tag="big", align_bytes=64)
+        nc.sync.dma_start(word_window[:], tab_words[0].rearrange("p t b -> p (t b)").bitcast(I32))
+        nc.sync.dma_start(wg8_codes[:], wg8_words[0].rearrange("p n b -> p (n b)").bitcast(I32))
+        nc.sync.dma_start(wg4_codes[:], wg4_words[0].bitcast(I32))
+        for q in range(4):
+            load_plane(wg8_plane, wg8_scales, q)
+        nc.sync.dma_start(wh_first[:, 0], wh_rows[0][:, :, 0:P])
+        for q in range(4):
+            load_plane(wg4_plane, wg4_scales, q)
+        nc.sync.dma_start(wh_first[:, 1], wh_rows[1][:, :, 0:P])
+        with nc.allow_non_contiguous_dma(reason="one bias value to a partition"):
+            nc.sync.dma_start(bias[:], bg.rearrange("(c p) -> p c", p=P))
+
+        carried = {}
+        wh_rest = {}
+
+        def load_carried(c):
+            carried[c] = stream.tile([P, T], F32, name=f"carried{c}", tag="big", align_bytes=64)
+            nc.sync.dma_start(carried[c][:], rT[c * P : (c + 1) * P, :])
+
+        def load_wh_rest(a):
+            wh_rest[a] = stream.tile([P, PACK, N - P], F32, name=f"wh_rest{a}", tag="big", align_bytes=64)
+            nc.sync.dma_start(wh_rest[a][:], wh_rows[a][:, :, P:N])
+
+        for c in range(3):
+            load_carried(c)
+
+        nc.scalar.mul(neg_bias[:], bias[:], -1.0)
+
+        def listed(h):
+            return offsets[:, h * HALF // GROUP : (h + 1) * HALF // GROUP]
+
+        nc.vector.tensor_copy(picked_scales[:], scale_window[:].bitcast(U8).indirect(offsets[:]))
+        for a in range(PASSES):
+            shift = LIVE + 4 * a
+            nc.scalar.dma_start(shifted_scales[0 : P - shift, a, :], picked_scales[:].bitcast(I32)[shift:P, :])
+        item_planes = [shifted_scales[:, a, :].bitcast(U8) for a in range(PASSES)]
+
+        item_codes = []
+        for h in range(HALVES):
+            picked_words = keep.tile([P, HALF], I32, name=f"picked_words{h}", align_bytes=64)
+            nc.vector.tensor_copy(picked_words[:].bitcast(U32), word_window[:].bitcast(U32).indirect(listed(h)))
+            parted = keep.tile([P, PASSES, HALF], U16, name=f"parted{h}", align_bytes=64)
+            nc.vector.tensor_copy(parted[:], picked_words[:].bitcast(U16).rearrange("p (j a) -> p a j", a=PASSES))
+            item_codes.append(parted)
+
+        def product(bank, h, weights):
+            acc = psum.tile([P, HALF], F32, name=f"bank{bank}")
+            for a, (codes, plane) in enumerate(weights):
+                nc.tensor.matmul_mx(
+                    out=acc[:],
+                    lhsT=codes,
+                    lhsT_scale=plane,
+                    rhs=item_codes[h][:, a, :].bitcast(FP4X4),
+                    rhs_scale=item_planes[a][:, h * HALF : (h + 1) * HALF],
+                    start=(a == 0),
+                    stop=(a == PASSES - 1),
+                )
+            return acc
+
+        wh_codes = keep.tile([P, CHUNKS, PASSES, P], U32, name="wh_codes", align_bytes=64)
+        wh_plane = keep.tile([P, CHUNKS, PASSES, P], U8, name="wh_plane", align_bytes=64)
+
+        def quantise_wh(c):
+            grouped = keep.tile([P, PASSES, P, PACK], BF16, name=f"grouped{c}", align_bytes=64)
+            for a in range(PASSES):
+                raw = wh_first[:, a] if c == 0 else wh_rest[a][:, :, (c - 1) * P : c * P]
+                nc.scalar.copy(grouped[:, a], raw.rearrange("p i n -> p n i"))
+            nc.vector.quantize_mx(
+                out=wh_codes[:, c].rearrange("p a n -> p (a n)").bitcast(FP8X4),
+                scales=wh_plane[:, c].rearrange("p a n -> p (a n)"),
+                in_=grouped[:].rearrange("p a n i -> p (a n i)"),
+            )
+
+        load_wh_rest(0)
+        quantise_wh(0)
+
+        carry_gate = [keep.tile([P, J], F32, name=f"carry_gate{c}") for c in range(CHUNKS)]
+        kept = [keep.tile([P, J], F32, name=f"kept{c}") for c in range(CHUNKS)]
+        for c in range(CHUNKS):
+            cols = slice(c * P, (c + 1) * P)
+            gate_weights = [
+                (wg8_codes[:, cols].bitcast(FP8X4), wg8_plane[:].bitcast(U8)[:, cols]),
+                (wg4_codes[:].bitcast(FP4X4)[:, cols], wg4_plane[:].bitcast(U8)[:, cols]),
+            ]
+            for h in range(HALVES):
+                acc = product(HALVES * c + h, h, gate_weights)
+                nc.scalar.activation(
+                    carry_gate[c][:, h * HALF : (h + 1) * HALF],
+                    acc[:],
+                    ACT.Sigmoid,
+                    bias=neg_bias[:, c : c + 1],
+                    scale=-1.0,
+                )
+
+        def carry(c):
+            if c == 0:
+                for h in range(HALVES):
+                    js = slice(h * HALF, (h + 1) * HALF)
+                    nc.vector.tensor_tensor(
+                        kept[c][:, js], carried[c][:].indirect(listed(h)), carry_gate[c][:, js], ALU.mult
+                    )
+            else:
+                nc.vector.tensor_tensor(kept[c][:], carried[c][:].indirect(offsets[:]), carry_gate[c][:], ALU.mult)
+
+        def transform(c):
+            wh_weights = [(wh_codes[:, c, a, :].bitcast(FP8X4), wh_plane[:, c, a, :]) for a in range(PASSES)]
+            made = []
+            for h in range(HALVES):
+                acc = product(HALVES * ((c - 1) % CHUNKS) + h, h, wh_weights)
+                silu = keep.tile([P, HALF], F32, name=f"silu{c}_{h}")
+                nc.scalar.activation(silu[:], acc[:], ACT.Silu)
+                made.append(silu)
+            return made
+
+        def combine(c, made):
+            gated = []
+            for h in range(HALVES):
+                neg_gated = ring.tile([P, HALF], F32, name="neg_gated")
+                nc.vector.scalar_tensor_tensor(
+                    neg_gated[:],
+                    carry_gate[c][:, h * HALF : (h + 1) * HALF],
+                    1.0,
+                    made[h][:],
+                    ALU.subtract,
+                    ALU.mult,
+                )
+                gated.append(neg_gated)
+            for h in range(HALVES):
+                js = slice(h * HALF, (h + 1) * HALF)
+                result = keep.tile([P, HALF], F32, name=f"result{c}_{h}")
+                nc.vector.tensor_tensor(result[:], kept[c][:, js], gated[h][:], ALU.subtract)
+                nc.sync.dma_start(out[c * P : (c + 1) * P, js], result[:])
+
+        carry(0)
+        load_wh_rest(1)
+        carry(1)
+        load_carried(3)
+        carry(2)
+        made0 = transform(0)
+        quantise_wh(1)
+        quantise_wh(2)
+        combine(0, made0)
+        made1 = transform(1)
+        quantise_wh(3)
+        carry(3)
+        made2 = transform(2)
+        made3 = transform(3)
+        combine(1, made1)
+        combine(2, made2)
+        combine(3, made3)

@@ -42,23 +42,24 @@ def tile_list_hwayt_mix_silu_kernel(
         shifted_scales = keep.tile([P, PASSES, J // 4], I32, name="shifted_scales", align_bytes=64)
         wg8_codes = keep.tile([P, N], I32, name="wg8_codes", align_bytes=64)
         wg4_codes = keep.tile([P, N // 2], I32, name="wg4_codes", align_bytes=64)
-        wg8_plane = keep.tile([P, N // 4], I32, name="wg8_plane", align_bytes=64)
-        wg4_plane = keep.tile([P, N // 4], I32, name="wg4_plane", align_bytes=64)
+        wg_planes = keep.tile([P, PASSES, N // 4], I32, name="wg_planes", align_bytes=64)
         wh_first = keep.tile([P, PASSES, PACK, P], F32, name="wh_first")
-        bias = keep.tile([P, CHUNKS], F32, name="bias")
+        bias_rows = keep.tile([P, 32], F32, name="bias_rows", align_bytes=64)
+        bias = keep.tile([P, 32], F32, name="bias", align_bytes=64)
         neg_bias = keep.tile([P, CHUNKS], F32, name="neg_bias")
         warm_in = keep.tile([P, 1], F32, name="warm_in")
         warm_out = keep.tile([P, 1], F32, name="warm_out")
 
+        nc.vector.memset(wg_planes[:], 0)
+        nc.vector.memset(bias_rows[:], 0.0)
+        nc.vector.memset(warm_in[:], 0.0)
         for q in range(4):
             nc.vector.memset(scale_window[32 * q : 32 * q + LIVE, :], 0)
-        nc.vector.memset(warm_in[:], 0.0)
         nc.vector.memset(shifted_scales[96:P], 0)
         nc.scalar.activation(warm_out[:], warm_in[:], ACT.Sigmoid)
 
-        def load_plane(plane, scales, q):
-            rows = scales[0].bitcast(I32)[4 * q : 4 * q + 4, :]
-            nc.sync.dma_start(plane[32 * q : 32 * (q + 1), :], rows.unsqueeze(0).to_broadcast([8, 4, N // 4]))
+        def load_plane(a, scales, q):
+            nc.sync.dma_start(wg_planes[32 * q : 32 * q + 4, a, :], scales[0].bitcast(I32)[4 * q : 4 * q + 4, :])
 
         wh_rows = wh.rearrange("(a p i) n -> a p i n", a=PASSES, i=PACK)
         nc.sync.dma_start(offsets[:], offs)
@@ -71,13 +72,12 @@ def tile_list_hwayt_mix_silu_kernel(
         nc.sync.dma_start(wg8_codes[:], wg8_words[0].rearrange("p n b -> p (n b)").bitcast(I32))
         nc.sync.dma_start(wg4_codes[:], wg4_words[0].bitcast(I32))
         for q in range(4):
-            load_plane(wg8_plane, wg8_scales, q)
+            load_plane(0, wg8_scales, q)
         nc.sync.dma_start(wh_first[:, 0], wh_rows[0][:, :, 0:P])
         for q in range(4):
-            load_plane(wg4_plane, wg4_scales, q)
+            load_plane(1, wg4_scales, q)
         nc.sync.dma_start(wh_first[:, 1], wh_rows[1][:, :, 0:P])
-        with nc.allow_non_contiguous_dma(reason="one bias value to a partition"):
-            nc.sync.dma_start(bias[:], bg.rearrange("(c p) -> p c", p=P))
+        nc.sync.dma_start(bias_rows[0:P:8, :], bg.rearrange("(c b i) -> b c i", c=CHUNKS, b=4))
 
         carried = {}
         wh_rest = {}
@@ -93,7 +93,6 @@ def tile_list_hwayt_mix_silu_kernel(
         for c in range(3):
             load_carried(c)
 
-        nc.scalar.mul(neg_bias[:], bias[:], -1.0)
 
         def listed(h):
             return offsets[:, h * HALF // GROUP : (h + 1) * HALF // GROUP]
@@ -140,6 +139,8 @@ def tile_list_hwayt_mix_silu_kernel(
                 in_=grouped[:].rearrange("p a n i -> p (a n i)"),
             )
 
+        nc.vector.transpose(bias[:], bias_rows[:])
+        nc.scalar.mul(neg_bias[:], bias[:, 0:32:8], -1.0)
         load_wh_rest(0)
         quantise_wh(0)
 
@@ -148,8 +149,8 @@ def tile_list_hwayt_mix_silu_kernel(
         for c in range(CHUNKS):
             cols = slice(c * P, (c + 1) * P)
             gate_weights = [
-                (wg8_codes[:, cols].bitcast(FP8X4), wg8_plane[:].bitcast(U8)[:, cols]),
-                (wg4_codes[:].bitcast(FP4X4)[:, cols], wg4_plane[:].bitcast(U8)[:, cols]),
+                (wg8_codes[:, cols].bitcast(FP8X4), wg_planes[:, 0, :].bitcast(U8)[:, cols]),
+                (wg4_codes[:].bitcast(FP4X4)[:, cols], wg_planes[:, 1, :].bitcast(U8)[:, cols]),
             ]
             for h in range(HALVES):
                 acc = product(HALVES * c + h, h, gate_weights)

@@ -23,7 +23,6 @@ CHUNKS = N // P
 HALF = 512
 HALVES = J // HALF
 GROUP = 16
-LIVE = 24
 
 
 def tile_list_hwayt_mix_silu_kernel(
@@ -32,84 +31,108 @@ def tile_list_hwayt_mix_silu_kernel(
     nc = tc.nc
     with ExitStack() as ctx:
         keep = ctx.enter_context(tc.tile_pool(name="keep", bufs=1))
-        ring = ctx.enter_context(tc.tile_pool(name="ring", bufs=3))
-        stream = ctx.enter_context(tc.tile_pool(name="stream", bufs=4))
+        ring = ctx.enter_context(tc.tile_pool(name="ring", bufs=4))
+        stream = ctx.enter_context(tc.tile_pool(name="stream", bufs=2))
         psum = ctx.enter_context(tc.psum_pool(name="psum", bufs=1))
 
         offsets = keep.tile([P, J // GROUP], U16, name="offsets")
         scale_window = keep.tile([P, T // 4], I32, name="scale_window", align_bytes=64)
         picked_scales = keep.tile([P, J], U8, name="picked_scales", align_bytes=64)
-        shifted_scales = keep.tile([P, PASSES, J // 4], I32, name="shifted_scales", align_bytes=64)
+        item_planes = [keep.tile([P, J // 4], I32, name=f"item_plane{a}", align_bytes=64) for a in range(PASSES)]
         wg8_codes = keep.tile([P, N], I32, name="wg8_codes", align_bytes=64)
         wg4_codes = keep.tile([P, N // 2], I32, name="wg4_codes", align_bytes=64)
         wg_planes = keep.tile([P, PASSES, N // 4], I32, name="wg_planes", align_bytes=64)
-        wh_first = keep.tile([P, PASSES, PACK, P], F32, name="wh_first")
         bias_rows = keep.tile([P, 32], F32, name="bias_rows", align_bytes=64)
         bias = keep.tile([P, 32], F32, name="bias", align_bytes=64)
-        neg_bias = keep.tile([P, CHUNKS], F32, name="neg_bias")
+        tanh_bias = keep.tile([P, CHUNKS], F32, name="tanh_bias")
         warm_in = keep.tile([P, 1], F32, name="warm_in")
         warm_out = keep.tile([P, 1], F32, name="warm_out")
 
-        nc.vector.memset(wg_planes[:], 0)
-        nc.vector.memset(bias_rows[:], 0.0)
         nc.vector.memset(warm_in[:], 0.0)
-        for q in range(4):
-            nc.vector.memset(scale_window[32 * q : 32 * q + LIVE, :], 0)
-        nc.vector.memset(shifted_scales[96:P], 0)
-        nc.scalar.activation(warm_out[:], warm_in[:], ACT.Sigmoid)
-
-        def load_plane(a, scales, q):
-            nc.sync.dma_start(wg_planes[32 * q : 32 * q + 4, a, :], scales[0].bitcast(I32)[4 * q : 4 * q + 4, :])
+        nc.scalar.activation(warm_out[:], warm_in[:], ACT.Silu)
+        nc.gpsimd.memset(bias_rows[:], 0.0)
+        nc.gpsimd.memset(wg_planes[:], 0)
+        nc.vector.memset(scale_window[0:16, :], 0)
+        nc.vector.memset(scale_window[32:48, :], 0)
+        nc.vector.memset(scale_window[64:P, :], 0)
 
         wh_rows = wh.rearrange("(a p i) n -> a p i n", a=PASSES, i=PACK)
-        nc.sync.dma_start(offsets[:], offs)
-        for q in range(4):
-            nc.sync.dma_start(
-                scale_window[32 * q + LIVE : 32 * (q + 1), :], tab_scales.bitcast(I32)[:, 4 * q : 4 * q + 4, :]
-            )
-        word_window = stream.tile([P, T], I32, name="word_window", tag="big", align_bytes=64)
-        nc.sync.dma_start(word_window[:], tab_words[0].rearrange("p t b -> p (t b)").bitcast(I32))
-        nc.sync.dma_start(wg8_codes[:], wg8_words[0].rearrange("p n b -> p (n b)").bitcast(I32))
-        nc.sync.dma_start(wg4_codes[:], wg4_words[0].bitcast(I32))
-        for q in range(4):
-            load_plane(0, wg8_scales, q)
-        nc.sync.dma_start(wh_first[:, 0], wh_rows[0][:, :, 0:P])
-        for q in range(4):
-            load_plane(1, wg4_scales, q)
-        nc.sync.dma_start(wh_first[:, 1], wh_rows[1][:, :, 0:P])
-        nc.sync.dma_start(bias_rows[0:P:8, :], bg.rearrange("(c b i) -> b c i", c=CHUNKS, b=4))
-
+        wh_raw = {}
         carried = {}
-        wh_rest = {}
+
+        def load_wh(c):
+            for a in range(PASSES):
+                wh_raw[c, a] = stream.tile([P, PACK, P], F32, name=f"wh_raw{c}_{a}", tag="wh_raw")
+                nc.sync.dma_start(wh_raw[c, a][:], wh_rows[a][:, :, c * P : (c + 1) * P])
 
         def load_carried(c):
             carried[c] = stream.tile([P, T], F32, name=f"carried{c}", tag="big", align_bytes=64)
             nc.sync.dma_start(carried[c][:], rT[c * P : (c + 1) * P, :])
 
-        def load_wh_rest(a):
-            wh_rest[a] = stream.tile([P, PACK, N - P], F32, name=f"wh_rest{a}", tag="big", align_bytes=64)
-            nc.sync.dma_start(wh_rest[a][:], wh_rows[a][:, :, P:N])
+        nc.sync.dma_start(offsets[:], offs)
+        scale_rows = tab_scales.rearrange("a (u x) t -> (a u) x t", u=2).bitcast(I32)
+        for q in range(2):
+            nc.sync.dma_start(scale_window[32 * q + 16 : 32 * q + 32, :], scale_rows[:, 4 * q : 4 * q + 4, :])
+        word_window = stream.tile([P, T], I32, name="word_window", tag="big", align_bytes=64)
+        nc.sync.dma_start(word_window[:], tab_words[0].rearrange("p t b -> p (t b)").bitcast(I32))
+        load_wh(0)
+        load_carried(0)
+        nc.sync.dma_start(wg8_codes[:], wg8_words[0].rearrange("p n b -> p (n b)").bitcast(I32))
+        nc.sync.dma_start(wg4_codes[:], wg4_words[0].bitcast(I32))
 
-        for c in range(3):
-            load_carried(c)
-
+        nc.gpsimd.dma_start(bias_rows[0:P:8, :], bg.rearrange("(c b i) -> b c i", c=CHUNKS, b=4))
+        for a, scales in enumerate((wg8_scales, wg4_scales)):
+            for q in range(4):
+                nc.gpsimd.dma_start(wg_planes[32 * q : 32 * q + 4, a, :], scales[0].bitcast(I32)[4 * q : 4 * q + 4, :])
 
         def listed(h):
             return offsets[:, h * HALF // GROUP : (h + 1) * HALF // GROUP]
 
         nc.vector.tensor_copy(picked_scales[:], scale_window[:].bitcast(U8).indirect(offsets[:]))
         for a in range(PASSES):
-            shift = LIVE + 4 * a
-            nc.scalar.dma_start(shifted_scales[0 : P - shift, a, :], picked_scales[:].bitcast(I32)[shift:P, :])
-        item_planes = [shifted_scales[:, a, :].bitcast(U8) for a in range(PASSES)]
+            for u in range(2):
+                first = 16 + 4 * (2 * a + u)
+                nc.scalar.dma_start(
+                    item_planes[a][64 * u : 64 * u + 64, :], picked_scales[:].bitcast(I32)[first : first + 64, :]
+                )
 
+        wh_codes = [keep.tile([P, PASSES, P], U32, name=f"wh_codes{c}", align_bytes=64) for c in range(CHUNKS)]
+        wh_plane = [keep.tile([P, PASSES, P], U8, name=f"wh_plane{c}", align_bytes=64) for c in range(CHUNKS)]
+        grouped = {}
+
+        def round_wh(c):
+            grouped[c] = keep.tile([P, PASSES, P, PACK], BF16, name=f"grouped{c}", align_bytes=64)
+            for a in range(PASSES):
+                nc.scalar.copy(grouped[c][:, a], wh_raw[c, a][:].rearrange("p i n -> p n i"))
+
+        def quantise_wh(c):
+            nc.vector.quantize_mx(
+                out=wh_codes[c][:].rearrange("p a n -> p (a n)").bitcast(FP8X4),
+                scales=wh_plane[c][:].rearrange("p a n -> p (a n)"),
+                in_=grouped[c][:].rearrange("p a n i -> p (a n i)"),
+            )
+
+        picked_words = []
         item_codes = []
-        for h in range(HALVES):
-            picked_words = keep.tile([P, HALF], I32, name=f"picked_words{h}", align_bytes=64)
-            nc.vector.tensor_copy(picked_words[:].bitcast(U32), word_window[:].bitcast(U32).indirect(listed(h)))
+
+        def pick_words(h):
+            picked = keep.tile([P, HALF], I32, name=f"picked_words{h}", align_bytes=64)
+            nc.vector.tensor_copy(picked[:].bitcast(U32), word_window[:].bitcast(U32).indirect(listed(h)))
+            picked_words.append(picked)
+
+        def part_words(h):
             parted = keep.tile([P, PASSES, HALF], U16, name=f"parted{h}", align_bytes=64)
-            nc.vector.tensor_copy(parted[:], picked_words[:].bitcast(U16).rearrange("p (j a) -> p a j", a=PASSES))
+            nc.vector.tensor_copy(parted[:], picked_words[h][:].bitcast(U16).rearrange("p (j a) -> p a j", a=PASSES))
             item_codes.append(parted)
+
+        round_wh(0)
+        pick_words(0)
+        pick_words(1)
+        quantise_wh(0)
+        part_words(0)
+        part_words(1)
+        nc.vector.transpose(bias[:], bias_rows[:])
+        nc.scalar.mul(tanh_bias[:], bias[:, 0:32:8], -0.5)
 
         def product(bank, h, weights):
             acc = psum.tile([P, HALF], F32, name=f"bank{bank}")
@@ -119,102 +142,59 @@ def tile_list_hwayt_mix_silu_kernel(
                     lhsT=codes,
                     lhsT_scale=plane,
                     rhs=item_codes[h][:, a, :].bitcast(FP4X4),
-                    rhs_scale=item_planes[a][:, h * HALF : (h + 1) * HALF],
+                    rhs_scale=item_planes[a][:].bitcast(U8)[:, h * HALF : (h + 1) * HALF],
                     start=(a == 0),
                     stop=(a == PASSES - 1),
                 )
             return acc
 
-        wh_codes = keep.tile([P, CHUNKS, PASSES, P], U32, name="wh_codes", align_bytes=64)
-        wh_plane = keep.tile([P, CHUNKS, PASSES, P], U8, name="wh_plane", align_bytes=64)
-
-        def quantise_wh(c):
-            grouped = keep.tile([P, PASSES, P, PACK], BF16, name=f"grouped{c}", align_bytes=64)
-            for a in range(PASSES):
-                raw = wh_first[:, a] if c == 0 else wh_rest[a][:, :, (c - 1) * P : c * P]
-                nc.scalar.copy(grouped[:, a], raw.rearrange("p i n -> p n i"))
-            nc.vector.quantize_mx(
-                out=wh_codes[:, c].rearrange("p a n -> p (a n)").bitcast(FP8X4),
-                scales=wh_plane[:, c].rearrange("p a n -> p (a n)"),
-                in_=grouped[:].rearrange("p a n i -> p (a n i)"),
-            )
-
-        nc.vector.transpose(bias[:], bias_rows[:])
-        nc.scalar.mul(neg_bias[:], bias[:, 0:32:8], -1.0)
-        load_wh_rest(0)
-        quantise_wh(0)
-
-        carry_gate = [keep.tile([P, J], F32, name=f"carry_gate{c}") for c in range(CHUNKS)]
-        kept = [keep.tile([P, J], F32, name=f"kept{c}") for c in range(CHUNKS)]
-        for c in range(CHUNKS):
-            cols = slice(c * P, (c + 1) * P)
-            gate_weights = [
-                (wg8_codes[:, cols].bitcast(FP8X4), wg_planes[:, 0, :].bitcast(U8)[:, cols]),
-                (wg4_codes[:].bitcast(FP4X4)[:, cols], wg_planes[:, 1, :].bitcast(U8)[:, cols]),
-            ]
-            for h in range(HALVES):
-                acc = product(HALVES * c + h, h, gate_weights)
-                nc.scalar.activation(
-                    carry_gate[c][:, h * HALF : (h + 1) * HALF],
-                    acc[:],
-                    ACT.Sigmoid,
-                    bias=neg_bias[:, c : c + 1],
-                    scale=-1.0,
-                )
-
-        def carry(c):
-            if c == 0:
-                for h in range(HALVES):
-                    js = slice(h * HALF, (h + 1) * HALF)
-                    nc.vector.tensor_tensor(
-                        kept[c][:, js], carried[c][:].indirect(listed(h)), carry_gate[c][:, js], ALU.mult
-                    )
-            else:
-                nc.vector.tensor_tensor(kept[c][:], carried[c][:].indirect(offsets[:]), carry_gate[c][:], ALU.mult)
-
         def transform(c):
-            wh_weights = [(wh_codes[:, c, a, :].bitcast(FP8X4), wh_plane[:, c, a, :]) for a in range(PASSES)]
+            weights = [(wh_codes[c][:, a, :].bitcast(FP8X4), wh_plane[c][:, a, :]) for a in range(PASSES)]
             made = []
             for h in range(HALVES):
-                acc = product(HALVES * ((c - 1) % CHUNKS) + h, h, wh_weights)
+                acc = product(4 * (c % 2) + h, h, weights)
                 silu = keep.tile([P, HALF], F32, name=f"silu{c}_{h}")
                 nc.scalar.activation(silu[:], acc[:], ACT.Silu)
                 made.append(silu)
             return made
 
-        def combine(c, made):
-            gated = []
+        def gate(c):
+            cols = slice(c * P, (c + 1) * P)
+            weights = [
+                (wg8_codes[:, cols].bitcast(FP8X4), wg_planes[:, 0, :].bitcast(U8)[:, cols]),
+                (wg4_codes[:].bitcast(FP4X4)[:, cols], wg_planes[:, 1, :].bitcast(U8)[:, cols]),
+            ]
+            leaning = []
             for h in range(HALVES):
-                neg_gated = ring.tile([P, HALF], F32, name="neg_gated")
-                nc.vector.scalar_tensor_tensor(
-                    neg_gated[:],
-                    carry_gate[c][:, h * HALF : (h + 1) * HALF],
-                    1.0,
-                    made[h][:],
-                    ALU.subtract,
-                    ALU.mult,
-                )
-                gated.append(neg_gated)
-            for h in range(HALVES):
-                js = slice(h * HALF, (h + 1) * HALF)
-                result = keep.tile([P, HALF], F32, name=f"result{c}_{h}")
-                nc.vector.tensor_tensor(result[:], kept[c][:, js], gated[h][:], ALU.subtract)
-                nc.sync.dma_start(out[c * P : (c + 1) * P, js], result[:])
+                acc = product(4 * (c % 2) + 2 + h, h, weights)
+                lean = keep.tile([P, HALF], F32, name=f"lean{c}_{h}")
+                nc.scalar.activation(lean[:], acc[:], ACT.Tanh, bias=tanh_bias[:, c : c + 1], scale=-0.5)
+                leaning.append(lean)
+            return leaning
 
-        carry(0)
-        load_wh_rest(1)
-        carry(1)
-        load_carried(3)
-        carry(2)
-        made0 = transform(0)
-        quantise_wh(1)
-        quantise_wh(2)
-        combine(0, made0)
-        made1 = transform(1)
-        quantise_wh(3)
-        carry(3)
-        made2 = transform(2)
-        made3 = transform(3)
-        combine(1, made1)
-        combine(2, made2)
-        combine(3, made3)
+        made = transform(0)
+        for c in range(CHUNKS):
+            if c + 1 < CHUNKS:
+                load_wh(c + 1)
+                load_carried(c + 1)
+                round_wh(c + 1)
+            leaning = gate(c)
+            apart = []
+            for h in range(HALVES):
+                diff = ring.tile([P, HALF], F32, name="diff")
+                nc.vector.tensor_tensor(diff[:], carried[c][:].indirect(listed(h)), made[h][:], ALU.subtract)
+                apart.append(diff)
+            if c + 1 < CHUNKS:
+                quantise_wh(c + 1)
+                made_next = transform(c + 1)
+            twice = []
+            for h in range(HALVES):
+                doubled = ring.tile([P, HALF], F32, name="doubled")
+                nc.vector.scalar_tensor_tensor(doubled[:], leaning[h][:], 1.0, apart[h][:], ALU.add, ALU.mult)
+                twice.append(doubled)
+            for h in range(HALVES):
+                result = keep.tile([P, HALF], F32, name=f"result{c}_{h}")
+                nc.vector.scalar_tensor_tensor(result[:], twice[h][:], 0.5, made[h][:], ALU.mult, ALU.add)
+                nc.sync.dma_start(out[c * P : (c + 1) * P, h * HALF : (h + 1) * HALF], result[:])
+            if c + 1 < CHUNKS:
+                made = made_next

@@ -32,107 +32,118 @@ def tile_list_hwayt_mix_silu_kernel(
     with ExitStack() as ctx:
         keep = ctx.enter_context(tc.tile_pool(name="keep", bufs=1))
         ring = ctx.enter_context(tc.tile_pool(name="ring", bufs=4))
-        stream = ctx.enter_context(tc.tile_pool(name="stream", bufs=2))
+        shared = ctx.enter_context(tc.tile_pool(name="shared", bufs=1))
         psum = ctx.enter_context(tc.psum_pool(name="psum", bufs=1))
 
+        def placed(shape, dtype, name, offset):
+            return shared.tile(shape, dtype, name=name, offset=offset, align_bytes=64)
+
+        at_scales = 0
+        at_first = 2048
+        at_codes = at_first + 2048
+        at_raw = at_codes + 2048 * CHUNKS
+
         offsets = keep.tile([P, J // GROUP], U16, name="offsets")
-        scale_window = keep.tile([P, T // 4], I32, name="scale_window", align_bytes=64)
+        scale_window = placed([P, T // 4], I32, "scale_window", at_scales)
+        word_window = keep.tile([P, T], I32, name="word_window", align_bytes=64)
         picked_scales = keep.tile([P, J], U8, name="picked_scales", align_bytes=64)
         item_planes = [keep.tile([P, J // 4], I32, name=f"item_plane{a}", align_bytes=64) for a in range(PASSES)]
         wg8_codes = keep.tile([P, N], I32, name="wg8_codes", align_bytes=64)
         wg4_codes = keep.tile([P, N // 2], I32, name="wg4_codes", align_bytes=64)
-        wg_planes = keep.tile([P, PASSES, N // 4], I32, name="wg_planes", align_bytes=64)
+        wg8_plane = keep.tile([P, N // 4], I32, name="wg8_plane", align_bytes=64)
+        wg4_plane = keep.tile([P, N // 4], I32, name="wg4_plane", align_bytes=64)
+        carried = [keep.tile([P, T], F32, name=f"carried{c}", align_bytes=64) for c in range(CHUNKS)]
         bias_rows = keep.tile([P, 32], F32, name="bias_rows", align_bytes=64)
-        bias = keep.tile([P, 32], F32, name="bias", align_bytes=64)
         tanh_bias = keep.tile([P, CHUNKS], F32, name="tanh_bias")
         warm_in = keep.tile([P, 1], F32, name="warm_in")
         warm_out = keep.tile([P, 1], F32, name="warm_out")
 
+        nc.gpsimd.memset(bias_rows[:], 0.0)
+        nc.gpsimd.memset(wg8_plane[:], 0)
+        nc.gpsimd.memset(wg4_plane[:], 0)
         nc.vector.memset(warm_in[:], 0.0)
         nc.scalar.activation(warm_out[:], warm_in[:], ACT.Silu)
-        nc.gpsimd.memset(bias_rows[:], 0.0)
-        nc.gpsimd.memset(wg_planes[:], 0)
         nc.vector.memset(scale_window[0:16, :], 0)
         nc.vector.memset(scale_window[32:48, :], 0)
         nc.vector.memset(scale_window[64:P, :], 0)
 
         wh_rows = wh.rearrange("(a p i) n -> a p i n", a=PASSES, i=PACK)
         wh_raw = {}
-        carried = {}
+
+        def load_plane(plane, scales):
+            for q in range(4):
+                nc.sync.dma_start(plane[32 * q : 32 * q + 4, :], scales[0].bitcast(I32)[4 * q : 4 * q + 4, :])
 
         def load_wh(c):
             for a in range(PASSES):
-                wh_raw[c, a] = stream.tile([P, PACK, P], F32, name=f"wh_raw{c}_{a}", tag="wh_raw")
+                wh_raw[c, a] = placed([P, PACK, P], F32, f"wh_raw{c}_{a}", at_raw + 5120 * c + 2048 * a)
                 nc.sync.dma_start(wh_raw[c, a][:], wh_rows[a][:, :, c * P : (c + 1) * P])
 
         def load_carried(c):
-            carried[c] = stream.tile([P, T], F32, name=f"carried{c}", tag="big", align_bytes=64)
             nc.sync.dma_start(carried[c][:], rT[c * P : (c + 1) * P, :])
 
         nc.sync.dma_start(offsets[:], offs)
         scale_rows = tab_scales.rearrange("a (u x) t -> (a u) x t", u=2).bitcast(I32)
         for q in range(2):
             nc.sync.dma_start(scale_window[32 * q + 16 : 32 * q + 32, :], scale_rows[:, 4 * q : 4 * q + 4, :])
-        word_window = stream.tile([P, T], I32, name="word_window", tag="big", align_bytes=64)
         nc.sync.dma_start(word_window[:], tab_words[0].rearrange("p t b -> p (t b)").bitcast(I32))
+        load_plane(wg8_plane, wg8_scales)
         load_wh(0)
-        load_carried(0)
         nc.sync.dma_start(wg8_codes[:], wg8_words[0].rearrange("p n b -> p (n b)").bitcast(I32))
         nc.sync.dma_start(wg4_codes[:], wg4_words[0].bitcast(I32))
-
         nc.gpsimd.dma_start(bias_rows[0:P:8, :], bg.rearrange("(c b i) -> b c i", c=CHUNKS, b=4))
-        for a, scales in enumerate((wg8_scales, wg4_scales)):
-            for q in range(4):
-                nc.gpsimd.dma_start(wg_planes[32 * q : 32 * q + 4, a, :], scales[0].bitcast(I32)[4 * q : 4 * q + 4, :])
 
         def listed(h):
             return offsets[:, h * HALF // GROUP : (h + 1) * HALF // GROUP]
 
         nc.vector.tensor_copy(picked_scales[:], scale_window[:].bitcast(U8).indirect(offsets[:]))
-        for a in range(PASSES):
-            for u in range(2):
-                first = 16 + 4 * (2 * a + u)
-                nc.scalar.dma_start(
-                    item_planes[a][64 * u : 64 * u + 64, :], picked_scales[:].bitcast(I32)[first : first + 64, :]
-                )
+        for a, u in ((0, 0), (1, 0), (1, 1), (0, 1)):
+            first = 16 + 4 * (2 * a + u)
+            nc.sync.dma_start(
+                item_planes[a][64 * u : 64 * u + 64, :], picked_scales[:].bitcast(I32)[first : first + 64, :]
+            )
+        bias = placed([P, 32], F32, "bias", at_scales)
+        nc.vector.transpose(bias[:], bias_rows[:])
+        nc.scalar.mul(tanh_bias[:], bias[:, 0:32:8], -0.5)
 
-        wh_codes = [keep.tile([P, PASSES, P], U32, name=f"wh_codes{c}", align_bytes=64) for c in range(CHUNKS)]
-        wh_plane = [keep.tile([P, PASSES, P], U8, name=f"wh_plane{c}", align_bytes=64) for c in range(CHUNKS)]
+        load_carried(0)
+        load_plane(wg4_plane, wg4_scales)
+        load_wh(1)
+        for c in range(1, CHUNKS):
+            load_carried(c)
+            if c + 1 < CHUNKS:
+                load_wh(c + 1)
+
+        wh_codes = {}
+        wh_plane = {}
         grouped = {}
 
         def round_wh(c):
-            grouped[c] = keep.tile([P, PASSES, P, PACK], BF16, name=f"grouped{c}", align_bytes=64)
+            grouped[c] = placed([P, PASSES, P, PACK], BF16, f"grouped{c}", at_codes + 2048 * (c - 1) if c else at_first)
             for a in range(PASSES):
                 nc.scalar.copy(grouped[c][:, a], wh_raw[c, a][:].rearrange("p i n -> p n i"))
 
         def quantise_wh(c):
+            wh_codes[c] = placed([P, PASSES, P], U32, f"wh_codes{c}", at_codes + 2048 * c)
+            wh_plane[c] = keep.tile([P, PASSES, P], U8, name=f"wh_plane{c}", align_bytes=64)
             nc.vector.quantize_mx(
                 out=wh_codes[c][:].rearrange("p a n -> p (a n)").bitcast(FP8X4),
                 scales=wh_plane[c][:].rearrange("p a n -> p (a n)"),
                 in_=grouped[c][:].rearrange("p a n i -> p (a n i)"),
             )
 
-        picked_words = []
         item_codes = []
 
-        def pick_words(h):
-            picked = keep.tile([P, HALF], I32, name=f"picked_words{h}", align_bytes=64)
+        def pick_words(h, picked):
             nc.vector.tensor_copy(picked[:].bitcast(U32), word_window[:].bitcast(U32).indirect(listed(h)))
-            picked_words.append(picked)
-
-        def part_words(h):
             parted = keep.tile([P, PASSES, HALF], U16, name=f"parted{h}", align_bytes=64)
-            nc.vector.tensor_copy(parted[:], picked_words[h][:].bitcast(U16).rearrange("p (j a) -> p a j", a=PASSES))
+            nc.vector.tensor_copy(parted[:], picked[:].bitcast(U16).rearrange("p (j a) -> p a j", a=PASSES))
             item_codes.append(parted)
 
         round_wh(0)
-        pick_words(0)
-        pick_words(1)
+        pick_words(0, keep.tile([P, HALF], I32, name="picked_words0", align_bytes=64))
         quantise_wh(0)
-        part_words(0)
-        part_words(1)
-        nc.vector.transpose(bias[:], bias_rows[:])
-        nc.scalar.mul(tanh_bias[:], bias[:, 0:32:8], -0.5)
+        pick_words(1, placed([P, HALF], I32, "picked_words1", at_first))
 
         def product(bank, h, weights):
             acc = psum.tile([P, HALF], F32, name=f"bank{bank}")
@@ -152,7 +163,7 @@ def tile_list_hwayt_mix_silu_kernel(
             weights = [(wh_codes[c][:, a, :].bitcast(FP8X4), wh_plane[c][:, a, :]) for a in range(PASSES)]
             made = []
             for h in range(HALVES):
-                acc = product(4 * (c % 2) + h, h, weights)
+                acc = product(HALVES * c + h, h, weights)
                 silu = keep.tile([P, HALF], F32, name=f"silu{c}_{h}")
                 nc.scalar.activation(silu[:], acc[:], ACT.Silu)
                 made.append(silu)
@@ -161,13 +172,16 @@ def tile_list_hwayt_mix_silu_kernel(
         def gate(c):
             cols = slice(c * P, (c + 1) * P)
             weights = [
-                (wg8_codes[:, cols].bitcast(FP8X4), wg_planes[:, 0, :].bitcast(U8)[:, cols]),
-                (wg4_codes[:].bitcast(FP4X4)[:, cols], wg_planes[:, 1, :].bitcast(U8)[:, cols]),
+                (wg8_codes[:, cols].bitcast(FP8X4), wg8_plane[:].bitcast(U8)[:, cols]),
+                (wg4_codes[:].bitcast(FP4X4)[:, cols], wg4_plane[:].bitcast(U8)[:, cols]),
             ]
             leaning = []
             for h in range(HALVES):
-                acc = product(4 * (c % 2) + 2 + h, h, weights)
-                lean = keep.tile([P, HALF], F32, name=f"lean{c}_{h}")
+                acc = product(HALVES * c + h, h, weights)
+                if c + 1 < CHUNKS:
+                    lean = placed([P, HALF], F32, f"lean{c}_{h}", at_raw + 5120 * (c + 1) + 1024 + 2048 * h)
+                else:
+                    lean = keep.tile([P, HALF], F32, name=f"lean{c}_{h}")
                 nc.scalar.activation(lean[:], acc[:], ACT.Tanh, bias=tanh_bias[:, c : c + 1], scale=-0.5)
                 leaning.append(lean)
             return leaning
@@ -175,8 +189,6 @@ def tile_list_hwayt_mix_silu_kernel(
         made = transform(0)
         for c in range(CHUNKS):
             if c + 1 < CHUNKS:
-                load_wh(c + 1)
-                load_carried(c + 1)
                 round_wh(c + 1)
             leaning = gate(c)
             apart = []
@@ -189,7 +201,10 @@ def tile_list_hwayt_mix_silu_kernel(
                 made_next = transform(c + 1)
             twice = []
             for h in range(HALVES):
-                doubled = ring.tile([P, HALF], F32, name="doubled")
+                if h == 0 and c + 1 < CHUNKS:
+                    doubled = placed([P, HALF], F32, f"doubled{c}", at_codes + 2048 * c)
+                else:
+                    doubled = ring.tile([P, HALF], F32, name="doubled")
                 nc.vector.scalar_tensor_tensor(doubled[:], leaning[h][:], 1.0, apart[h][:], ALU.add, ALU.mult)
                 twice.append(doubled)
             for h in range(HALVES):

@@ -38,13 +38,9 @@ def tile_list_hwayt_mix_silu_kernel(
         def placed(shape, dtype, name, offset):
             return shared.tile(shape, dtype, name=name, offset=offset, align_bytes=64)
 
-        at_scales = 0
-        at_first = 2048
-        at_codes = at_first + 2048
-        at_raw = at_codes + 2048 * CHUNKS
 
         offsets = keep.tile([P, J // GROUP], U16, name="offsets")
-        scale_window = placed([P, T // 4], I32, "scale_window", at_scales)
+        scale_window = keep.tile([P, T // 4], I32, name="scale_window", align_bytes=64)
         word_window = keep.tile([P, T], I32, name="word_window", align_bytes=64)
         picked_scales = keep.tile([P, J], U8, name="picked_scales", align_bytes=64)
         item_planes = [keep.tile([P, J // 4], I32, name=f"item_plane{a}", align_bytes=64) for a in range(PASSES)]
@@ -76,7 +72,7 @@ def tile_list_hwayt_mix_silu_kernel(
 
         def load_wh(c):
             for a in range(PASSES):
-                wh_raw[c, a] = placed([P, PACK, P], F32, f"wh_raw{c}_{a}", at_raw + 5120 * c + 2048 * a)
+                wh_raw[c, a] = placed([P, PACK, P], F32, f"wh_raw{c}_{a}", 2048 * (PASSES * c + a))
                 nc.sync.dma_start(wh_raw[c, a][:], wh_rows[a][:, :, c * P : (c + 1) * P])
 
         def load_carried(c):
@@ -89,8 +85,7 @@ def tile_list_hwayt_mix_silu_kernel(
         nc.sync.dma_start(word_window[:], tab_words[0].rearrange("p t b -> p (t b)").bitcast(I32))
         load_plane(wg8_plane, wg8_scales)
         load_wh(0)
-        nc.sync.dma_start(wg8_codes[:], wg8_words[0].rearrange("p n b -> p (n b)").bitcast(I32))
-        nc.sync.dma_start(wg4_codes[:], wg4_words[0].bitcast(I32))
+        load_wh(1)
         nc.gpsimd.dma_start(bias_rows[0:P:8, :], bg.rearrange("(c b i) -> b c i", c=CHUNKS, b=4))
 
         def listed(h):
@@ -102,29 +97,27 @@ def tile_list_hwayt_mix_silu_kernel(
             nc.sync.dma_start(
                 item_planes[a][64 * u : 64 * u + 64, :], picked_scales[:].bitcast(I32)[first : first + 64, :]
             )
-        bias = placed([P, 32], F32, "bias", at_scales)
-        nc.vector.transpose(bias[:], bias_rows[:])
-        nc.scalar.mul(tanh_bias[:], bias[:, 0:32:8], -0.5)
 
         load_carried(0)
+        nc.sync.dma_start(wg8_codes[:], wg8_words[0].rearrange("p n b -> p (n b)").bitcast(I32))
+        nc.sync.dma_start(wg4_codes[:], wg4_words[0].bitcast(I32))
         load_plane(wg4_plane, wg4_scales)
-        load_wh(1)
         for c in range(1, CHUNKS):
-            load_carried(c)
             if c + 1 < CHUNKS:
                 load_wh(c + 1)
+            load_carried(c)
 
         wh_codes = {}
         wh_plane = {}
         grouped = {}
 
         def round_wh(c):
-            grouped[c] = placed([P, PASSES, P, PACK], BF16, f"grouped{c}", at_codes + 2048 * (c - 1) if c else at_first)
+            grouped[c] = keep.tile([P, PASSES, P, PACK], BF16, name=f"grouped{c}", align_bytes=64)
             for a in range(PASSES):
                 nc.scalar.copy(grouped[c][:, a], wh_raw[c, a][:].rearrange("p i n -> p n i"))
 
         def quantise_wh(c):
-            wh_codes[c] = placed([P, PASSES, P], U32, f"wh_codes{c}", at_codes + 2048 * c)
+            wh_codes[c] = keep.tile([P, PASSES, P], U32, name=f"wh_codes{c}", align_bytes=64)
             wh_plane[c] = keep.tile([P, PASSES, P], U8, name=f"wh_plane{c}", align_bytes=64)
             nc.vector.quantize_mx(
                 out=wh_codes[c][:].rearrange("p a n -> p (a n)").bitcast(FP8X4),
@@ -141,9 +134,14 @@ def tile_list_hwayt_mix_silu_kernel(
             item_codes.append(parted)
 
         round_wh(0)
+        round_wh(1)
         pick_words(0, keep.tile([P, HALF], I32, name="picked_words0", align_bytes=64))
         quantise_wh(0)
-        pick_words(1, placed([P, HALF], I32, "picked_words1", at_first))
+        pick_words(1, placed([P, HALF], I32, "picked_words1", 2048))
+        quantise_wh(1)
+        bias = placed([P, 32], F32, "bias", 2048 * 3)
+        nc.vector.transpose(bias[:], bias_rows[:])
+        nc.scalar.mul(tanh_bias[:], bias[:, 0:32:8], -0.5)
 
         def product(bank, h, weights):
             acc = psum.tile([P, HALF], F32, name=f"bank{bank}")
@@ -178,38 +176,35 @@ def tile_list_hwayt_mix_silu_kernel(
             leaning = []
             for h in range(HALVES):
                 acc = product(HALVES * c + h, h, weights)
-                if c + 1 < CHUNKS:
-                    lean = placed([P, HALF], F32, f"lean{c}_{h}", at_raw + 5120 * (c + 1) + 1024 + 2048 * h)
-                else:
-                    lean = keep.tile([P, HALF], F32, name=f"lean{c}_{h}")
+                lean = keep.tile([P, HALF], F32, name=f"lean{c}_{h}")
                 nc.scalar.activation(lean[:], acc[:], ACT.Tanh, bias=tanh_bias[:, c : c + 1], scale=-0.5)
                 leaning.append(lean)
             return leaning
 
-        made = transform(0)
+        made = {0: transform(0), 1: transform(1)}
         for c in range(CHUNKS):
-            if c + 1 < CHUNKS:
-                round_wh(c + 1)
             leaning = gate(c)
+            if c + 2 < CHUNKS:
+                round_wh(c + 2)
             apart = []
             for h in range(HALVES):
                 diff = ring.tile([P, HALF], F32, name="diff")
-                nc.vector.tensor_tensor(diff[:], carried[c][:].indirect(listed(h)), made[h][:], ALU.subtract)
+                nc.vector.tensor_tensor(diff[:], carried[c][:].indirect(listed(h)), made[c][h][:], ALU.subtract)
                 apart.append(diff)
-            if c + 1 < CHUNKS:
-                quantise_wh(c + 1)
-                made_next = transform(c + 1)
             twice = []
             for h in range(HALVES):
-                if h == 0 and c + 1 < CHUNKS:
-                    doubled = placed([P, HALF], F32, f"doubled{c}", at_codes + 2048 * c)
-                else:
-                    doubled = ring.tile([P, HALF], F32, name="doubled")
+                doubled = ring.tile([P, HALF], F32, name="doubled")
                 nc.vector.scalar_tensor_tensor(doubled[:], leaning[h][:], 1.0, apart[h][:], ALU.add, ALU.mult)
                 twice.append(doubled)
+            if c + 2 < CHUNKS:
+                quantise_wh(c + 2)
+                made[c + 2] = transform(c + 2)
             for h in range(HALVES):
-                result = keep.tile([P, HALF], F32, name=f"result{c}_{h}")
-                nc.vector.scalar_tensor_tensor(result[:], twice[h][:], 0.5, made[h][:], ALU.mult, ALU.add)
-                nc.sync.dma_start(out[c * P : (c + 1) * P, h * HALF : (h + 1) * HALF], result[:])
-            if c + 1 < CHUNKS:
-                made = made_next
+                pieces = 2 if (c, h) == (CHUNKS - 1, HALVES - 1) else 1
+                width = HALF // pieces
+                for k in range(pieces):
+                    js = slice(k * width, (k + 1) * width)
+                    result = keep.tile([P, width], F32, name=f"result{c}_{h}_{k}")
+                    nc.vector.scalar_tensor_tensor(result[:], twice[h][:, js], 0.5, made[c][h][:, js], ALU.mult, ALU.add)
+                    first = h * HALF + k * width
+                    nc.sync.dma_start(out[c * P : (c + 1) * P, first : first + width], result[:])

@@ -66,14 +66,13 @@ def tile_list_hwayt_mix_silu_kernel(
         wh_rows = wh.rearrange("(a p i) n -> a p i n", a=PASSES, i=PACK)
         wh_raw = {}
 
-        def load_plane(plane, scales):
+        def load_plane(queue, plane, scales):
             for q in range(4):
-                nc.sync.dma_start(plane[32 * q : 32 * q + 4, :], scales[0].bitcast(I32)[4 * q : 4 * q + 4, :])
+                queue.dma_start(plane[32 * q : 32 * q + 4, :], scales[0].bitcast(I32)[4 * q : 4 * q + 4, :])
 
-        def load_wh(c):
-            for a in range(PASSES):
-                wh_raw[c, a] = placed([P, PACK, P], F32, f"wh_raw{c}_{a}", 2048 * (PASSES * c + a))
-                nc.sync.dma_start(wh_raw[c, a][:], wh_rows[a][:, :, c * P : (c + 1) * P])
+        def load_wh(c, a):
+            wh_raw[c, a] = placed([P, PACK, P], F32, f"wh_raw{c}_{a}", 2048 * (PASSES * c + a))
+            nc.sync.dma_start(wh_raw[c, a][:], wh_rows[a][:, :, c * P : (c + 1) * P])
 
         def load_carried(c):
             nc.sync.dma_start(carried[c][:], rT[c * P : (c + 1) * P, :])
@@ -83,10 +82,10 @@ def tile_list_hwayt_mix_silu_kernel(
         for q in range(2):
             nc.sync.dma_start(scale_window[32 * q + 16 : 32 * q + 32, :], scale_rows[:, 4 * q : 4 * q + 4, :])
         nc.sync.dma_start(word_window[:], tab_words[0].rearrange("p t b -> p (t b)").bitcast(I32))
-        load_plane(wg8_plane, wg8_scales)
-        load_wh(0)
-        load_wh(1)
+        load_wh(0, 0)
+        load_wh(0, 1)
         nc.gpsimd.dma_start(bias_rows[0:P:8, :], bg.rearrange("(c b i) -> b c i", c=CHUNKS, b=4))
+        load_plane(nc.gpsimd, wg8_plane, wg8_scales)
 
         def listed(h):
             return offsets[:, h * HALF // GROUP : (h + 1) * HALF // GROUP]
@@ -94,18 +93,21 @@ def tile_list_hwayt_mix_silu_kernel(
         nc.vector.tensor_copy(picked_scales[:], scale_window[:].bitcast(U8).indirect(offsets[:]))
         for a, u in ((0, 0), (1, 0), (1, 1), (0, 1)):
             first = 16 + 4 * (2 * a + u)
-            nc.sync.dma_start(
+            nc.scalar.dma_start(
                 item_planes[a][64 * u : 64 * u + 64, :], picked_scales[:].bitcast(I32)[first : first + 64, :]
             )
 
         load_carried(0)
         nc.sync.dma_start(wg8_codes[:], wg8_words[0].rearrange("p n b -> p (n b)").bitcast(I32))
         nc.sync.dma_start(wg4_codes[:], wg4_words[0].bitcast(I32))
-        load_plane(wg4_plane, wg4_scales)
+        load_wh(1, 0)
+        load_plane(nc.sync, wg4_plane, wg4_scales)
+        load_wh(1, 1)
         for c in range(1, CHUNKS):
-            if c + 1 < CHUNKS:
-                load_wh(c + 1)
             load_carried(c)
+            if c + 1 < CHUNKS:
+                load_wh(c + 1, 0)
+                load_wh(c + 1, 1)
 
         wh_codes = {}
         wh_plane = {}
@@ -134,12 +136,10 @@ def tile_list_hwayt_mix_silu_kernel(
             item_codes.append(parted)
 
         round_wh(0)
-        round_wh(1)
         pick_words(0, keep.tile([P, HALF], I32, name="picked_words0", align_bytes=64))
         quantise_wh(0)
         pick_words(1, placed([P, HALF], I32, "picked_words1", 2048))
-        quantise_wh(1)
-        bias = placed([P, 32], F32, "bias", 2048 * 3)
+        bias = placed([P, 32], F32, "bias", 0)
         nc.vector.transpose(bias[:], bias_rows[:])
         nc.scalar.mul(tanh_bias[:], bias[:, 0:32:8], -0.5)
 
@@ -181,24 +181,27 @@ def tile_list_hwayt_mix_silu_kernel(
                 leaning.append(lean)
             return leaning
 
-        made = {0: transform(0), 1: transform(1)}
+        made = {0: transform(0)}
         for c in range(CHUNKS):
             leaning = gate(c)
-            if c + 2 < CHUNKS:
-                round_wh(c + 2)
+            if c + 1 < CHUNKS:
+                round_wh(c + 1)
             apart = []
             for h in range(HALVES):
                 diff = ring.tile([P, HALF], F32, name="diff")
                 nc.vector.tensor_tensor(diff[:], carried[c][:].indirect(listed(h)), made[c][h][:], ALU.subtract)
                 apart.append(diff)
+            if c + 1 < CHUNKS:
+                quantise_wh(c + 1)
+                made[c + 1] = transform(c + 1)
             twice = []
             for h in range(HALVES):
-                doubled = ring.tile([P, HALF], F32, name="doubled")
+                if h == 0 and 0 < c < CHUNKS - 1:
+                    doubled = placed([P, HALF], F32, f"doubled{c}", 2048 * (PASSES * (c + 1) + 1))
+                else:
+                    doubled = ring.tile([P, HALF], F32, name="doubled")
                 nc.vector.scalar_tensor_tensor(doubled[:], leaning[h][:], 1.0, apart[h][:], ALU.add, ALU.mult)
                 twice.append(doubled)
-            if c + 2 < CHUNKS:
-                quantise_wh(c + 2)
-                made[c + 2] = transform(c + 2)
             for h in range(HALVES):
                 pieces = 2 if (c, h) == (CHUNKS - 1, HALVES - 1) else 1
                 width = HALF // pieces

@@ -39,6 +39,9 @@ def tile_list_hwayt_mix_silu_kernel(
             return shared.tile(shape, dtype, name=name, offset=offset, align_bytes=64)
 
 
+        def raw_at(c, a):
+            return 5120 * c + 2048 * a
+
         offsets = keep.tile([P, J // GROUP], U16, name="offsets")
         scale_window = keep.tile([P, T // 4], I32, name="scale_window", align_bytes=64)
         word_window = keep.tile([P, T], I32, name="word_window", align_bytes=64)
@@ -54,11 +57,11 @@ def tile_list_hwayt_mix_silu_kernel(
         warm_in = keep.tile([P, 1], F32, name="warm_in")
         warm_out = keep.tile([P, 1], F32, name="warm_out")
 
-        nc.gpsimd.memset(bias_rows[:], 0.0)
-        nc.gpsimd.memset(wg8_plane[:], 0)
-        nc.gpsimd.memset(wg4_plane[:], 0)
         nc.vector.memset(warm_in[:], 0.0)
         nc.scalar.activation(warm_out[:], warm_in[:], ACT.Silu)
+        nc.vector.memset(wg8_plane[:], 0)
+        nc.vector.memset(bias_rows[:], 0.0)
+        nc.vector.memset(wg4_plane[:], 0)
         nc.vector.memset(scale_window[0:16, :], 0)
         nc.vector.memset(scale_window[32:48, :], 0)
         nc.vector.memset(scale_window[64:P, :], 0)
@@ -66,12 +69,12 @@ def tile_list_hwayt_mix_silu_kernel(
         wh_rows = wh.rearrange("(a p i) n -> a p i n", a=PASSES, i=PACK)
         wh_raw = {}
 
-        def load_plane(queue, plane, scales):
+        def load_plane(plane, scales):
             for q in range(4):
-                queue.dma_start(plane[32 * q : 32 * q + 4, :], scales[0].bitcast(I32)[4 * q : 4 * q + 4, :])
+                nc.sync.dma_start(plane[32 * q : 32 * q + 4, :], scales[0].bitcast(I32)[4 * q : 4 * q + 4, :])
 
         def load_wh(c, a):
-            wh_raw[c, a] = placed([P, PACK, P], F32, f"wh_raw{c}_{a}", 2048 * (PASSES * c + a))
+            wh_raw[c, a] = placed([P, PACK, P], F32, f"wh_raw{c}_{a}", raw_at(c, a))
             nc.sync.dma_start(wh_raw[c, a][:], wh_rows[a][:, :, c * P : (c + 1) * P])
 
         def load_carried(c):
@@ -82,10 +85,12 @@ def tile_list_hwayt_mix_silu_kernel(
         for q in range(2):
             nc.sync.dma_start(scale_window[32 * q + 16 : 32 * q + 32, :], scale_rows[:, 4 * q : 4 * q + 4, :])
         nc.sync.dma_start(word_window[:], tab_words[0].rearrange("p t b -> p (t b)").bitcast(I32))
+        load_plane(wg8_plane, wg8_scales)
+        nc.sync.dma_start(bias_rows[0:P:8, :], bg.rearrange("(c b i) -> b c i", c=CHUNKS, b=4))
         load_wh(0, 0)
         load_wh(0, 1)
-        nc.gpsimd.dma_start(bias_rows[0:P:8, :], bg.rearrange("(c b i) -> b c i", c=CHUNKS, b=4))
-        load_plane(nc.gpsimd, wg8_plane, wg8_scales)
+        nc.sync.dma_start(wg8_codes[:], wg8_words[0].rearrange("p n b -> p (n b)").bitcast(I32))
+        nc.sync.dma_start(wg4_codes[:], wg4_words[0].bitcast(I32))
 
         def listed(h):
             return offsets[:, h * HALF // GROUP : (h + 1) * HALF // GROUP]
@@ -93,21 +98,17 @@ def tile_list_hwayt_mix_silu_kernel(
         nc.vector.tensor_copy(picked_scales[:], scale_window[:].bitcast(U8).indirect(offsets[:]))
         for a, u in ((0, 0), (1, 0), (1, 1), (0, 1)):
             first = 16 + 4 * (2 * a + u)
-            nc.scalar.dma_start(
+            nc.sync.dma_start(
                 item_planes[a][64 * u : 64 * u + 64, :], picked_scales[:].bitcast(I32)[first : first + 64, :]
             )
 
         load_carried(0)
-        nc.sync.dma_start(wg8_codes[:], wg8_words[0].rearrange("p n b -> p (n b)").bitcast(I32))
-        nc.sync.dma_start(wg4_codes[:], wg4_words[0].bitcast(I32))
-        load_wh(1, 0)
-        load_plane(nc.sync, wg4_plane, wg4_scales)
-        load_wh(1, 1)
         for c in range(1, CHUNKS):
+            load_wh(c, 0)
+            load_wh(c, 1)
+            if c == 1:
+                load_plane(wg4_plane, wg4_scales)
             load_carried(c)
-            if c + 1 < CHUNKS:
-                load_wh(c + 1, 0)
-                load_wh(c + 1, 1)
 
         wh_codes = {}
         wh_plane = {}
@@ -138,8 +139,8 @@ def tile_list_hwayt_mix_silu_kernel(
         round_wh(0)
         pick_words(0, keep.tile([P, HALF], I32, name="picked_words0", align_bytes=64))
         quantise_wh(0)
-        pick_words(1, placed([P, HALF], I32, "picked_words1", 2048))
-        bias = placed([P, 32], F32, "bias", 0)
+        pick_words(1, placed([P, HALF], I32, "picked_words1", raw_at(0, 1) + 128))
+        bias = placed([P, 32], F32, "bias", raw_at(0, 1))
         nc.vector.transpose(bias[:], bias_rows[:])
         nc.scalar.mul(tanh_bias[:], bias[:, 0:32:8], -0.5)
 
@@ -161,7 +162,7 @@ def tile_list_hwayt_mix_silu_kernel(
             weights = [(wh_codes[c][:, a, :].bitcast(FP8X4), wh_plane[c][:, a, :]) for a in range(PASSES)]
             made = []
             for h in range(HALVES):
-                acc = product(HALVES * c + h, h, weights)
+                acc = product(HALVES * max(c - 1, 0) + h, h, weights)
                 silu = keep.tile([P, HALF], F32, name=f"silu{c}_{h}")
                 nc.scalar.activation(silu[:], acc[:], ACT.Silu)
                 made.append(silu)
@@ -175,17 +176,20 @@ def tile_list_hwayt_mix_silu_kernel(
             ]
             leaning = []
             for h in range(HALVES):
-                acc = product(HALVES * c + h, h, weights)
-                lean = keep.tile([P, HALF], F32, name=f"lean{c}_{h}")
+                acc = product(HALVES * max(c - 1, 0) + h, h, weights)
+                if c + 1 < CHUNKS:
+                    lean = placed([P, HALF], F32, f"lean{c}_{h}", raw_at(c + 1, h) + 1024)
+                else:
+                    lean = keep.tile([P, HALF], F32, name=f"lean{c}_{h}")
                 nc.scalar.activation(lean[:], acc[:], ACT.Tanh, bias=tanh_bias[:, c : c + 1], scale=-0.5)
                 leaning.append(lean)
             return leaning
 
         made = {0: transform(0)}
         for c in range(CHUNKS):
-            leaning = gate(c)
             if c + 1 < CHUNKS:
                 round_wh(c + 1)
+            leaning = gate(c)
             apart = []
             for h in range(HALVES):
                 diff = ring.tile([P, HALF], F32, name="diff")
@@ -196,10 +200,7 @@ def tile_list_hwayt_mix_silu_kernel(
                 made[c + 1] = transform(c + 1)
             twice = []
             for h in range(HALVES):
-                if h == 0 and 0 < c < CHUNKS - 1:
-                    doubled = placed([P, HALF], F32, f"doubled{c}", 2048 * (PASSES * (c + 1) + 1))
-                else:
-                    doubled = ring.tile([P, HALF], F32, name="doubled")
+                doubled = ring.tile([P, HALF], F32, name="doubled")
                 nc.vector.scalar_tensor_tensor(doubled[:], leaning[h][:], 1.0, apart[h][:], ALU.add, ALU.mult)
                 twice.append(doubled)
             for h in range(HALVES):

@@ -38,9 +38,8 @@ def tile_list_hwayt_mix_silu_kernel(
         def placed(shape, dtype, name, offset):
             return shared.tile(shape, dtype, name=name, offset=offset, align_bytes=64)
 
-
         def raw_at(c, a):
-            return 5120 * c + 2048 * a
+            return 4096 * a if c < 2 else 8192 + 5120 * (c - 2) + 2048 * a
 
         offsets = keep.tile([P, J // GROUP], U16, name="offsets")
         scale_window = keep.tile([P, T // 4], I32, name="scale_window", align_bytes=64)
@@ -73,9 +72,12 @@ def tile_list_hwayt_mix_silu_kernel(
             for q in range(4):
                 nc.sync.dma_start(plane[32 * q : 32 * q + 4, :], scales[0].bitcast(I32)[4 * q : 4 * q + 4, :])
 
-        def load_wh(c, a):
-            wh_raw[c, a] = placed([P, PACK, P], F32, f"wh_raw{c}_{a}", raw_at(c, a))
-            nc.sync.dma_start(wh_raw[c, a][:], wh_rows[a][:, :, c * P : (c + 1) * P])
+        def load_wh(first, count):
+            for a in range(PASSES):
+                raw = placed([P, PACK, count * P], F32, f"wh_raw{first}_{a}", raw_at(first, a))
+                nc.sync.dma_start(raw[:], wh_rows[a][:, :, first * P : (first + count) * P])
+                for k in range(count):
+                    wh_raw[first + k, a] = raw[:, :, k * P : (k + 1) * P]
 
         def load_carried(c):
             nc.sync.dma_start(carried[c][:], rT[c * P : (c + 1) * P, :])
@@ -87,10 +89,7 @@ def tile_list_hwayt_mix_silu_kernel(
         nc.sync.dma_start(word_window[:], tab_words[0].rearrange("p t b -> p (t b)").bitcast(I32))
         load_plane(wg8_plane, wg8_scales)
         nc.sync.dma_start(bias_rows[0:P:8, :], bg.rearrange("(c b i) -> b c i", c=CHUNKS, b=4))
-        load_wh(0, 0)
-        load_wh(0, 1)
-        nc.sync.dma_start(wg8_codes[:], wg8_words[0].rearrange("p n b -> p (n b)").bitcast(I32))
-        nc.sync.dma_start(wg4_codes[:], wg4_words[0].bitcast(I32))
+        load_wh(0, 2)
 
         def listed(h):
             return offsets[:, h * HALF // GROUP : (h + 1) * HALF // GROUP]
@@ -103,11 +102,12 @@ def tile_list_hwayt_mix_silu_kernel(
             )
 
         load_carried(0)
-        for c in range(1, CHUNKS):
-            load_wh(c, 0)
+        nc.sync.dma_start(wg8_codes[:], wg8_words[0].rearrange("p n b -> p (n b)").bitcast(I32))
+        nc.sync.dma_start(wg4_codes[:], wg4_words[0].bitcast(I32))
+        load_plane(wg4_plane, wg4_scales)
+        load_carried(1)
+        for c in range(2, CHUNKS):
             load_wh(c, 1)
-            if c == 1:
-                load_plane(wg4_plane, wg4_scales)
             load_carried(c)
 
         wh_codes = {}
@@ -117,30 +117,36 @@ def tile_list_hwayt_mix_silu_kernel(
         def round_wh(c):
             grouped[c] = keep.tile([P, PASSES, P, PACK], BF16, name=f"grouped{c}", align_bytes=64)
             for a in range(PASSES):
-                nc.scalar.copy(grouped[c][:, a], wh_raw[c, a][:].rearrange("p i n -> p n i"))
+                nc.scalar.copy(grouped[c][:, a], wh_raw[c, a].rearrange("p i n -> p n i"))
 
-        def quantise_wh(c):
+        for c in range(CHUNKS):
             wh_codes[c] = keep.tile([P, PASSES, P], U32, name=f"wh_codes{c}", align_bytes=64)
             wh_plane[c] = keep.tile([P, PASSES, P], U8, name=f"wh_plane{c}", align_bytes=64)
+
+        def quantise_wh(c, passes):
             nc.vector.quantize_mx(
-                out=wh_codes[c][:].rearrange("p a n -> p (a n)").bitcast(FP8X4),
-                scales=wh_plane[c][:].rearrange("p a n -> p (a n)"),
-                in_=grouped[c][:].rearrange("p a n i -> p (a n i)"),
+                out=wh_codes[c][:, passes].rearrange("p a n -> p (a n)").bitcast(FP8X4),
+                scales=wh_plane[c][:, passes].rearrange("p a n -> p (a n)"),
+                in_=grouped[c][:, passes].rearrange("p a n i -> p (a n i)"),
             )
 
+        picked_words = [keep.tile([P, HALF], I32, name=f"picked_words{h}", align_bytes=64) for h in range(HALVES)]
         item_codes = []
 
-        def pick_words(h, picked):
-            nc.vector.tensor_copy(picked[:].bitcast(U32), word_window[:].bitcast(U32).indirect(listed(h)))
-            parted = keep.tile([P, PASSES, HALF], U16, name=f"parted{h}", align_bytes=64)
-            nc.vector.tensor_copy(parted[:], picked[:].bitcast(U16).rearrange("p (j a) -> p a j", a=PASSES))
+        def part_words(h, parted):
+            nc.vector.tensor_copy(parted[:], picked_words[h][:].bitcast(U16).rearrange("p (j a) -> p a j", a=PASSES))
             item_codes.append(parted)
 
         round_wh(0)
-        pick_words(0, keep.tile([P, HALF], I32, name="picked_words0", align_bytes=64))
-        quantise_wh(0)
-        pick_words(1, placed([P, HALF], I32, "picked_words1", raw_at(0, 1) + 128))
-        bias = placed([P, 32], F32, "bias", raw_at(0, 1))
+        round_wh(1)
+        for h in range(HALVES):
+            nc.vector.tensor_copy(picked_words[h][:].bitcast(U32), word_window[:].bitcast(U32).indirect(listed(h)))
+        part_words(0, keep.tile([P, PASSES, HALF], U16, name="parted0", align_bytes=64))
+        for a in range(PASSES):
+            quantise_wh(0, slice(a, a + 1))
+        part_words(1, placed([P, PASSES, HALF], U16, "parted1", raw_at(0, 1)))
+        quantise_wh(1, slice(0, PASSES))
+        bias = placed([P, 32], F32, "bias", raw_at(0, 1) + 2048)
         nc.vector.transpose(bias[:], bias_rows[:])
         nc.scalar.mul(tanh_bias[:], bias[:, 0:32:8], -0.5)
 
@@ -177,7 +183,7 @@ def tile_list_hwayt_mix_silu_kernel(
             leaning = []
             for h in range(HALVES):
                 acc = product(HALVES * max(c - 1, 0) + h, h, weights)
-                if c + 1 < CHUNKS:
+                if 0 < c < CHUNKS - 1:
                     lean = placed([P, HALF], F32, f"lean{c}_{h}", raw_at(c + 1, h) + 1024)
                 else:
                     lean = keep.tile([P, HALF], F32, name=f"lean{c}_{h}")
@@ -187,7 +193,7 @@ def tile_list_hwayt_mix_silu_kernel(
 
         made = {0: transform(0)}
         for c in range(CHUNKS):
-            if c + 1 < CHUNKS:
+            if 0 < c < CHUNKS - 1:
                 round_wh(c + 1)
             leaning = gate(c)
             apart = []
@@ -195,8 +201,9 @@ def tile_list_hwayt_mix_silu_kernel(
                 diff = ring.tile([P, HALF], F32, name="diff")
                 nc.vector.tensor_tensor(diff[:], carried[c][:].indirect(listed(h)), made[c][h][:], ALU.subtract)
                 apart.append(diff)
+            if 0 < c < CHUNKS - 1:
+                quantise_wh(c + 1, slice(0, PASSES))
             if c + 1 < CHUNKS:
-                quantise_wh(c + 1)
                 made[c + 1] = transform(c + 1)
             twice = []
             for h in range(HALVES):

@@ -53,11 +53,7 @@ def tile_list_hwayt_mix_silu_kernel(
         carried = [keep.tile([P, T], F32, name=f"carried{c}", align_bytes=64) for c in range(CHUNKS)]
         bias_rows = keep.tile([P, 32], F32, name="bias_rows", align_bytes=64)
         tanh_bias = keep.tile([P, CHUNKS], F32, name="tanh_bias")
-        warm_in = keep.tile([P, 1], F32, name="warm_in")
-        warm_out = keep.tile([P, 1], F32, name="warm_out")
 
-        nc.vector.memset(warm_in[:], 0.0)
-        nc.scalar.activation(warm_out[:], warm_in[:], ACT.Silu)
         nc.vector.memset(wg8_plane[:], 0)
         nc.vector.memset(bias_rows[:], 0.0)
         nc.vector.memset(wg4_plane[:], 0)
@@ -117,7 +113,10 @@ def tile_list_hwayt_mix_silu_kernel(
         def round_wh(c):
             grouped[c] = keep.tile([P, PASSES, P, PACK], BF16, name=f"grouped{c}", align_bytes=64)
             for a in range(PASSES):
-                nc.scalar.copy(grouped[c][:, a], wh_raw[c, a].rearrange("p i n -> p n i"))
+                nc.scalar.copy(
+                    grouped[c][:, a].rearrange("p (m v) i -> p m i v", v=4),
+                    wh_raw[c, a].rearrange("p i (m v) -> p m i v", v=4),
+                )
 
         for c in range(CHUNKS):
             wh_codes[c] = keep.tile([P, PASSES, P], U32, name=f"wh_codes{c}", align_bytes=64)

@@ -78,10 +78,10 @@ def tile_list_hwayt_mix_silu_kernel(
         def load_carried(c):
             nc.sync.dma_start(carried[c][:], rT[c * P : (c + 1) * P, :])
 
-        nc.sync.dma_start(offsets[:], offs)
         scale_rows = tab_scales.rearrange("a (u x) t -> (a u) x t", u=2).bitcast(I32)
         for q in range(2):
             nc.sync.dma_start(scale_window[32 * q + 16 : 32 * q + 32, :], scale_rows[:, 4 * q : 4 * q + 4, :])
+        nc.sync.dma_start(offsets[:], offs)
         nc.sync.dma_start(word_window[:], tab_words[0].rearrange("p t b -> p (t b)").bitcast(I32))
         load_plane(wg8_plane, wg8_scales)
         nc.sync.dma_start(bias_rows[0:P:8, :], bg.rearrange("(c b i) -> b c i", c=CHUNKS, b=4))
@@ -101,9 +101,9 @@ def tile_list_hwayt_mix_silu_kernel(
         nc.sync.dma_start(wg8_codes[:], wg8_words[0].rearrange("p n b -> p (n b)").bitcast(I32))
         nc.sync.dma_start(wg4_codes[:], wg4_words[0].bitcast(I32))
         load_plane(wg4_plane, wg4_scales)
-        load_carried(1)
-        for c in range(2, CHUNKS):
-            load_wh(c, 1)
+        for c in range(1, CHUNKS):
+            if c + 1 < CHUNKS:
+                load_wh(c + 1, 1)
             load_carried(c)
 
         wh_codes = {}

@@ -18,11 +18,17 @@ ALU = mybir.AluOpType
 
 P = 128
 PACK = 4
-PASSES = 2
+PASSES = K // (P * PACK)
 CHUNKS = N // P
 HALF = 512
 HALVES = J // HALF
 GROUP = 16
+QUADRANT = 32
+SCALE_ROWS = 4
+TAIL = 16
+EARLY = 2
+RUN = 4
+LAST_PIECES = 2
 
 
 def tile_list_hwayt_mix_silu_kernel(
@@ -32,14 +38,8 @@ def tile_list_hwayt_mix_silu_kernel(
     with ExitStack() as ctx:
         keep = ctx.enter_context(tc.tile_pool(name="keep", bufs=1))
         ring = ctx.enter_context(tc.tile_pool(name="ring", bufs=4))
-        shared = ctx.enter_context(tc.tile_pool(name="shared", bufs=1))
+        reused = ctx.enter_context(tc.tile_pool(name="reused", bufs=1))
         psum = ctx.enter_context(tc.psum_pool(name="psum", bufs=1))
-
-        def placed(shape, dtype, name, offset):
-            return shared.tile(shape, dtype, name=name, offset=offset, align_bytes=64)
-
-        def raw_at(c, a):
-            return 4096 * a if c < 2 else 8192 + 5120 * (c - 2) + 2048 * a
 
         offsets = keep.tile([P, J // GROUP], U16, name="offsets")
         scale_window = keep.tile([P, T // 4], I32, name="scale_window", align_bytes=64)
@@ -51,50 +51,60 @@ def tile_list_hwayt_mix_silu_kernel(
         wg8_plane = keep.tile([P, N // 4], I32, name="wg8_plane", align_bytes=64)
         wg4_plane = keep.tile([P, N // 4], I32, name="wg4_plane", align_bytes=64)
         carried = [keep.tile([P, T], F32, name=f"carried{c}", align_bytes=64) for c in range(CHUNKS)]
-        bias_rows = keep.tile([P, 32], F32, name="bias_rows", align_bytes=64)
+        bias_rows = keep.tile([P, QUADRANT], F32, name="bias_rows", align_bytes=64)
         tanh_bias = keep.tile([P, CHUNKS], F32, name="tanh_bias")
 
         nc.vector.memset(wg8_plane[:], 0)
         nc.vector.memset(bias_rows[:], 0.0)
         nc.vector.memset(wg4_plane[:], 0)
-        nc.vector.memset(scale_window[0:16, :], 0)
-        nc.vector.memset(scale_window[32:48, :], 0)
-        nc.vector.memset(scale_window[64:P, :], 0)
+        nc.vector.memset(scale_window[0:TAIL, :], 0)
+        nc.vector.memset(scale_window[QUADRANT : QUADRANT + TAIL, :], 0)
+        nc.vector.memset(scale_window[2 * QUADRANT : P, :], 0)
+
+        def load_plane(plane, scales):
+            rows = scales[0].bitcast(I32)
+            for q in range(P // QUADRANT):
+                nc.sync.dma_start(
+                    plane[QUADRANT * q : QUADRANT * q + SCALE_ROWS, :], rows[SCALE_ROWS * q : SCALE_ROWS * (q + 1), :]
+                )
 
         wh_rows = wh.rearrange("(a p i) n -> a p i n", a=PASSES, i=PACK)
         wh_raw = {}
+        early_bytes = PACK * EARLY * P * 4
 
-        def load_plane(plane, scales):
-            for q in range(4):
-                nc.sync.dma_start(plane[32 * q : 32 * q + 4, :], scales[0].bitcast(I32)[4 * q : 4 * q + 4, :])
-
-        def load_wh(first, count):
+        def load_wh(tiles, first, count):
             for a in range(PASSES):
-                raw = placed([P, PACK, count * P], F32, f"wh_raw{first}_{a}", raw_at(first, a))
-                nc.sync.dma_start(raw[:], wh_rows[a][:, :, first * P : (first + count) * P])
+                nc.sync.dma_start(tiles[a][:], wh_rows[a][:, :, first * P : (first + count) * P])
                 for k in range(count):
-                    wh_raw[first + k, a] = raw[:, :, k * P : (k + 1) * P]
+                    wh_raw[first + k, a] = tiles[a][:, :, k * P : (k + 1) * P]
 
         def load_carried(c):
             nc.sync.dma_start(carried[c][:], rT[c * P : (c + 1) * P, :])
 
-        scale_rows = tab_scales.rearrange("a (u x) t -> (a u) x t", u=2).bitcast(I32)
-        for q in range(2):
-            nc.sync.dma_start(scale_window[32 * q + 16 : 32 * q + 32, :], scale_rows[:, 4 * q : 4 * q + 4, :])
-        nc.sync.dma_start(offsets[:], offs)
-        nc.sync.dma_start(word_window[:], tab_words[0].rearrange("p t b -> p (t b)").bitcast(I32))
-        load_plane(wg8_plane, wg8_scales)
-        nc.sync.dma_start(bias_rows[0:P:8, :], bg.rearrange("(c b i) -> b c i", c=CHUNKS, b=4))
-        load_wh(0, 2)
-
         def listed(h):
             return offsets[:, h * HALF // GROUP : (h + 1) * HALF // GROUP]
 
+        scale_rows = tab_scales.rearrange("a (u x) t -> (a u) x t", u=2).bitcast(I32)
+        for q in range(2):
+            nc.sync.dma_start(
+                scale_window[QUADRANT * q + TAIL : QUADRANT * (q + 1), :],
+                scale_rows[:, SCALE_ROWS * q : SCALE_ROWS * (q + 1), :],
+            )
+        nc.sync.dma_start(offsets[:], offs)
+        nc.sync.dma_start(word_window[:], tab_words[0].rearrange("p t b -> p (t b)").bitcast(I32))
+        load_plane(wg8_plane, wg8_scales)
+        nc.sync.dma_start(bias_rows[0:P:8, :], bg.rearrange("(c b i) -> b c i", c=CHUNKS, b=P // QUADRANT))
+        early_wh = [
+            reused.tile([P, PACK, EARLY * P], F32, name=f"early_wh{a}", offset=a * early_bytes, align_bytes=64)
+            for a in range(PASSES)
+        ]
+        load_wh(early_wh, 0, EARLY)
+
         nc.vector.tensor_copy(picked_scales[:], scale_window[:].bitcast(U8).indirect(offsets[:]))
         for a, u in ((0, 0), (1, 0), (1, 1), (0, 1)):
-            first = 16 + 4 * (2 * a + u)
+            source = TAIL + SCALE_ROWS * (2 * a + u)
             nc.sync.dma_start(
-                item_planes[a][64 * u : 64 * u + 64, :], picked_scales[:].bitcast(I32)[first : first + 64, :]
+                item_planes[a][64 * u : 64 * (u + 1), :], picked_scales[:].bitcast(I32)[source : source + 64, :]
             )
 
         load_carried(0)
@@ -103,31 +113,35 @@ def tile_list_hwayt_mix_silu_kernel(
         load_plane(wg4_plane, wg4_scales)
         for c in range(1, CHUNKS):
             if c + 1 < CHUNKS:
-                load_wh(c + 1, 1)
+                late_wh = [keep.tile([P, PACK, P], F32, name=f"late_wh{c + 1}_{a}") for a in range(PASSES)]
+                load_wh(late_wh, c + 1, 1)
             load_carried(c)
 
+        grouped = {}
         wh_codes = {}
         wh_plane = {}
-        grouped = {}
 
         def round_wh(c):
-            grouped[c] = keep.tile([P, PASSES, P, PACK], BF16, name=f"grouped{c}", align_bytes=64)
+            grouped[c] = keep.tile([P, PASSES, P, PACK], BF16, name=f"grouped{c}", tag=f"staged{c}", align_bytes=64)
             for a in range(PASSES):
                 nc.scalar.copy(
-                    grouped[c][:, a].rearrange("p (m v) i -> p m i v", v=4),
-                    wh_raw[c, a].rearrange("p i (m v) -> p m i v", v=4),
+                    grouped[c][:, a].rearrange("p (m v) i -> p m i v", v=RUN),
+                    wh_raw[c, a].rearrange("p i (m v) -> p m i v", v=RUN),
                 )
 
-        for c in range(CHUNKS):
-            wh_codes[c] = keep.tile([P, PASSES, P], U32, name=f"wh_codes{c}", align_bytes=64)
+        def quantise_wh(c, calls):
+            tag = f"staged{c + 1}" if c > 0 else "first_codes"
+            wh_codes[c] = keep.tile([P, PASSES, P], U32, name=f"wh_codes{c}", tag=tag, align_bytes=64)
             wh_plane[c] = keep.tile([P, PASSES, P], U8, name=f"wh_plane{c}", align_bytes=64)
+            for passes in calls:
+                nc.vector.quantize_mx(
+                    out=wh_codes[c][:, passes].rearrange("p a n -> p (a n)").bitcast(FP8X4),
+                    scales=wh_plane[c][:, passes].rearrange("p a n -> p (a n)"),
+                    in_=grouped[c][:, passes].rearrange("p a n i -> p (a n i)"),
+                )
 
-        def quantise_wh(c, passes):
-            nc.vector.quantize_mx(
-                out=wh_codes[c][:, passes].rearrange("p a n -> p (a n)").bitcast(FP8X4),
-                scales=wh_plane[c][:, passes].rearrange("p a n -> p (a n)"),
-                in_=grouped[c][:, passes].rearrange("p a n i -> p (a n i)"),
-            )
+        each_pass = [slice(a, a + 1) for a in range(PASSES)]
+        both_passes = [slice(0, PASSES)]
 
         picked_words = [keep.tile([P, HALF], I32, name=f"picked_words{h}", align_bytes=64) for h in range(HALVES)]
         item_codes = []
@@ -136,21 +150,21 @@ def tile_list_hwayt_mix_silu_kernel(
             nc.vector.tensor_copy(parted[:], picked_words[h][:].bitcast(U16).rearrange("p (j a) -> p a j", a=PASSES))
             item_codes.append(parted)
 
-        round_wh(0)
-        round_wh(1)
+        for c in range(EARLY):
+            round_wh(c)
         for h in range(HALVES):
             nc.vector.tensor_copy(picked_words[h][:].bitcast(U32), word_window[:].bitcast(U32).indirect(listed(h)))
         part_words(0, keep.tile([P, PASSES, HALF], U16, name="parted0", align_bytes=64))
-        for a in range(PASSES):
-            quantise_wh(0, slice(a, a + 1))
-        part_words(1, placed([P, PASSES, HALF], U16, "parted1", raw_at(0, 1)))
-        quantise_wh(1, slice(0, PASSES))
-        bias = placed([P, 32], F32, "bias", raw_at(0, 1) + 2048)
+        quantise_wh(0, each_pass)
+        part_words(1, reused.tile([P, PASSES, HALF], U16, name="parted1", offset=early_bytes, align_bytes=64))
+        quantise_wh(1, both_passes)
+        parted_bytes = PASSES * HALF * 2
+        bias = reused.tile([P, QUADRANT], F32, name="bias", offset=early_bytes + parted_bytes, align_bytes=64)
         nc.vector.transpose(bias[:], bias_rows[:])
-        nc.scalar.mul(tanh_bias[:], bias[:, 0:32:8], -0.5)
+        nc.scalar.mul(tanh_bias[:], bias[:, 0:QUADRANT:8], -0.5)
 
-        def product(bank, h, weights):
-            acc = psum.tile([P, HALF], F32, name=f"bank{bank}")
+        def product(c, h, weights):
+            acc = psum.tile([P, HALF], F32, name=f"bank{HALVES * max(c - 1, 0) + h}")
             for a, (codes, plane) in enumerate(weights):
                 nc.tensor.matmul_mx(
                     out=acc[:],
@@ -165,13 +179,13 @@ def tile_list_hwayt_mix_silu_kernel(
 
         def transform(c):
             weights = [(wh_codes[c][:, a, :].bitcast(FP8X4), wh_plane[c][:, a, :]) for a in range(PASSES)]
-            made = []
+            halves = []
             for h in range(HALVES):
-                acc = product(HALVES * max(c - 1, 0) + h, h, weights)
+                acc = product(c, h, weights)
                 silu = keep.tile([P, HALF], F32, name=f"silu{c}_{h}")
                 nc.scalar.activation(silu[:], acc[:], ACT.Silu)
-                made.append(silu)
-            return made
+                halves.append(silu)
+            return halves
 
         def gate(c):
             cols = slice(c * P, (c + 1) * P)
@@ -179,42 +193,40 @@ def tile_list_hwayt_mix_silu_kernel(
                 (wg8_codes[:, cols].bitcast(FP8X4), wg8_plane[:].bitcast(U8)[:, cols]),
                 (wg4_codes[:].bitcast(FP4X4)[:, cols], wg4_plane[:].bitcast(U8)[:, cols]),
             ]
-            leaning = []
+            halves = []
             for h in range(HALVES):
-                acc = product(HALVES * max(c - 1, 0) + h, h, weights)
-                if 0 < c < CHUNKS - 1:
-                    lean = placed([P, HALF], F32, f"lean{c}_{h}", raw_at(c + 1, h) + 1024)
-                else:
-                    lean = keep.tile([P, HALF], F32, name=f"lean{c}_{h}")
-                nc.scalar.activation(lean[:], acc[:], ACT.Tanh, bias=tanh_bias[:, c : c + 1], scale=-0.5)
-                leaning.append(lean)
-            return leaning
+                acc = product(c, h, weights)
+                tanh = keep.tile([P, HALF], F32, name=f"tanh{c}_{h}")
+                nc.scalar.activation(tanh[:], acc[:], ACT.Tanh, bias=tanh_bias[:, c : c + 1], scale=-0.5)
+                halves.append(tanh)
+            return halves
 
-        made = {0: transform(0)}
+        silus = {0: transform(0)}
         for c in range(CHUNKS):
-            if 0 < c < CHUNKS - 1:
+            late_next = EARLY <= c + 1 < CHUNKS
+            if late_next:
                 round_wh(c + 1)
-            leaning = gate(c)
-            apart = []
+            tanhs = gate(c)
+            diffs = []
             for h in range(HALVES):
                 diff = ring.tile([P, HALF], F32, name="diff")
-                nc.vector.tensor_tensor(diff[:], carried[c][:].indirect(listed(h)), made[c][h][:], ALU.subtract)
-                apart.append(diff)
-            if 0 < c < CHUNKS - 1:
-                quantise_wh(c + 1, slice(0, PASSES))
+                nc.vector.tensor_tensor(diff[:], carried[c][:].indirect(listed(h)), silus[c][h][:], ALU.subtract)
+                diffs.append(diff)
+            if late_next:
+                quantise_wh(c + 1, both_passes)
             if c + 1 < CHUNKS:
-                made[c + 1] = transform(c + 1)
-            twice = []
+                silus[c + 1] = transform(c + 1)
+            gated = []
             for h in range(HALVES):
-                doubled = ring.tile([P, HALF], F32, name="doubled")
-                nc.vector.scalar_tensor_tensor(doubled[:], leaning[h][:], 1.0, apart[h][:], ALU.add, ALU.mult)
-                twice.append(doubled)
+                twice = ring.tile([P, HALF], F32, name="twice")
+                nc.vector.scalar_tensor_tensor(twice[:], tanhs[h][:], 1.0, diffs[h][:], ALU.add, ALU.mult)
+                gated.append(twice)
             for h in range(HALVES):
-                pieces = 2 if (c, h) == (CHUNKS - 1, HALVES - 1) else 1
+                pieces = LAST_PIECES if (c, h) == (CHUNKS - 1, HALVES - 1) else 1
                 width = HALF // pieces
                 for k in range(pieces):
                     js = slice(k * width, (k + 1) * width)
                     result = keep.tile([P, width], F32, name=f"result{c}_{h}_{k}")
-                    nc.vector.scalar_tensor_tensor(result[:], twice[h][:, js], 0.5, made[c][h][:, js], ALU.mult, ALU.add)
-                    first = h * HALF + k * width
-                    nc.sync.dma_start(out[c * P : (c + 1) * P, first : first + width], result[:])
+                    nc.vector.scalar_tensor_tensor(result[:], gated[h][:, js], 0.5, silus[c][h][:, js], ALU.mult, ALU.add)
+                    column = h * HALF + k * width
+                    nc.sync.dma_start(out[c * P : (c + 1) * P, column : column + width], result[:])

@@ -1,6 +1,7 @@
 from contextlib import ExitStack
 
 import concourse.mybir as mybir
+from concourse.masks import make_identity
 
 K, N, T, J = 1024, 512, 2048, 1024
 FLOPS = 2 * 2 * K * N * J
@@ -28,6 +29,7 @@ SCALE_ROWS = 4
 TAIL = 16
 EARLY = 2
 RUN = 4
+TURNED = (1, 2)
 LAST_PIECES = 2
 
 
@@ -37,7 +39,7 @@ def tile_list_hwayt_mix_silu_kernel(
     nc = tc.nc
     with ExitStack() as ctx:
         keep = ctx.enter_context(tc.tile_pool(name="keep", bufs=1))
-        ring = ctx.enter_context(tc.tile_pool(name="ring", bufs=4))
+        ring = ctx.enter_context(tc.tile_pool(name="ring", bufs=6))
         reused = ctx.enter_context(tc.tile_pool(name="reused", bufs=1))
         psum = ctx.enter_context(tc.psum_pool(name="psum", bufs=1))
 
@@ -53,6 +55,8 @@ def tile_list_hwayt_mix_silu_kernel(
         carried = [keep.tile([P, T], F32, name=f"carried{c}", align_bytes=64) for c in range(CHUNKS)]
         bias_rows = keep.tile([P, QUADRANT], F32, name="bias_rows", align_bytes=64)
         tanh_bias = keep.tile([P, CHUNKS], F32, name="tanh_bias")
+        identity = keep.tile([P, P], F32, name="identity")
+        make_identity(nc, identity[:])
 
         nc.vector.memset(wg8_plane[:], 0)
         nc.vector.memset(bias_rows[:], 0.0)
@@ -60,6 +64,9 @@ def tile_list_hwayt_mix_silu_kernel(
         nc.vector.memset(scale_window[0:TAIL, :], 0)
         nc.vector.memset(scale_window[QUADRANT : QUADRANT + TAIL, :], 0)
         nc.vector.memset(scale_window[2 * QUADRANT : P, :], 0)
+
+        warm = keep.tile([P, 1], F32, name="warm")
+        nc.scalar.activation(warm[:], bias_rows[:, 0:1], ACT.Silu)
 
         def load_plane(plane, scales):
             rows = scales[0].bitcast(I32)
@@ -78,8 +85,8 @@ def tile_list_hwayt_mix_silu_kernel(
                 for k in range(count):
                     wh_raw[first + k, a] = tiles[a][:, :, k * P : (k + 1) * P]
 
-        def load_carried(c):
-            nc.sync.dma_start(carried[c][:], rT[c * P : (c + 1) * P, :])
+        def load_carried(c, cols=slice(0, T)):
+            nc.sync.dma_start(carried[c][:, cols], rT[c * P : (c + 1) * P, cols])
 
         def listed(h):
             return offsets[:, h * HALF // GROUP : (h + 1) * HALF // GROUP]
@@ -108,21 +115,22 @@ def tile_list_hwayt_mix_silu_kernel(
             )
 
         load_carried(0)
-        nc.sync.dma_start(wg8_codes[:], wg8_words[0].rearrange("p n b -> p (n b)").bitcast(I32))
-        nc.sync.dma_start(wg4_codes[:], wg4_words[0].bitcast(I32))
         load_plane(wg4_plane, wg4_scales)
+        nc.sync.dma_start(wg4_codes[:], wg4_words[0].bitcast(I32))
+        nc.sync.dma_start(wg8_codes[:], wg8_words[0].rearrange("p n b -> p (n b)").bitcast(I32))
+        load_carried(1, slice(0, T // 2))
         for c in range(1, CHUNKS):
             if c + 1 < CHUNKS:
                 late_wh = [keep.tile([P, PACK, P], F32, name=f"late_wh{c + 1}_{a}") for a in range(PASSES)]
                 load_wh(late_wh, c + 1, 1)
-            load_carried(c)
+            load_carried(c, slice(T // 2 if c == 1 else 0, T))
 
         grouped = {}
         wh_codes = {}
         wh_plane = {}
 
         def round_wh(c):
-            grouped[c] = keep.tile([P, PASSES, P, PACK], BF16, name=f"grouped{c}", tag=f"staged{c}", align_bytes=64)
+            grouped[c] = keep.tile([P, PASSES, P, PACK], BF16, name=f"grouped{c}", align_bytes=64)
             for a in range(PASSES):
                 nc.scalar.copy(
                     grouped[c][:, a].rearrange("p (m v) i -> p m i v", v=RUN),
@@ -130,8 +138,7 @@ def tile_list_hwayt_mix_silu_kernel(
                 )
 
         def quantise_wh(c, calls):
-            tag = f"staged{c + 1}" if c > 0 else "first_codes"
-            wh_codes[c] = keep.tile([P, PASSES, P], U32, name=f"wh_codes{c}", tag=tag, align_bytes=64)
+            wh_codes[c] = keep.tile([P, PASSES, P], U32, name=f"wh_codes{c}", align_bytes=64)
             wh_plane[c] = keep.tile([P, PASSES, P], U8, name=f"wh_plane{c}", align_bytes=64)
             for passes in calls:
                 nc.vector.quantize_mx(
@@ -163,8 +170,8 @@ def tile_list_hwayt_mix_silu_kernel(
         nc.vector.transpose(bias[:], bias_rows[:])
         nc.scalar.mul(tanh_bias[:], bias[:, 0:QUADRANT:8], -0.5)
 
-        def product(c, h, weights):
-            acc = psum.tile([P, HALF], F32, name=f"bank{HALVES * max(c - 1, 0) + h}")
+        def product(kind, h, weights):
+            acc = psum.tile([P, HALF], F32, name=f"{kind}{h}")
             for a, (codes, plane) in enumerate(weights):
                 nc.tensor.matmul_mx(
                     out=acc[:],
@@ -181,7 +188,7 @@ def tile_list_hwayt_mix_silu_kernel(
             weights = [(wh_codes[c][:, a, :].bitcast(FP8X4), wh_plane[c][:, a, :]) for a in range(PASSES)]
             halves = []
             for h in range(HALVES):
-                acc = product(c, h, weights)
+                acc = product("back" if c == 1 else "wh_sum", h, weights)
                 silu = keep.tile([P, HALF], F32, name=f"silu{c}_{h}")
                 nc.scalar.activation(silu[:], acc[:], ACT.Silu)
                 halves.append(silu)
@@ -195,38 +202,83 @@ def tile_list_hwayt_mix_silu_kernel(
             ]
             halves = []
             for h in range(HALVES):
-                acc = product(c, h, weights)
+                acc = product("turned" if c == 0 else "gate_sum", h, weights)
                 tanh = keep.tile([P, HALF], F32, name=f"tanh{c}_{h}")
                 nc.scalar.activation(tanh[:], acc[:], ACT.Tanh, bias=tanh_bias[:, c : c + 1], scale=-0.5)
                 halves.append(tanh)
             return halves
 
-        silus = {0: transform(0)}
-        for c in range(CHUNKS):
-            late_next = EARLY <= c + 1 < CHUNKS
-            if late_next:
-                round_wh(c + 1)
-            tanhs = gate(c)
+        def turned_sum(h, twice, silu):
+            total = psum.tile([P, HALF], F32, name=f"turned{h}")
+            terms = [silu, silu, twice]
+            for n, term in enumerate(terms):
+                for b in range(HALF // P):
+                    cols = slice(b * P, (b + 1) * P)
+                    nc.tensor.matmul(
+                        total[:, cols],
+                        lhsT=term[:, cols],
+                        rhs=identity[:],
+                        is_transpose=True,
+                        start=(n == 0 and b == 0),
+                        stop=(n == len(terms) - 1 and b == HALF // P - 1),
+                    )
+            halved = ring.tile([P, HALF], F32, name="halved")
+            nc.scalar.mul(halved[:], total[:], 0.5)
+            return halved
+
+        def turn_back(c, h, halved):
+            back = psum.tile([P, HALF], F32, name=f"back{h}")
+            for b in range(HALF // P):
+                cols = slice(b * P, (b + 1) * P)
+                nc.tensor.transpose(back[:, cols], halved[:, cols], identity[:])
+            result = keep.tile([P, HALF], F32, name=f"result{c}_{h}")
+            nc.scalar.copy(result[:], back[:])
+            nc.sync.dma_start(out[c * P : (c + 1) * P, h * HALF : (h + 1) * HALF], result[:])
+
+        def blend(c):
             diffs = []
             for h in range(HALVES):
                 diff = ring.tile([P, HALF], F32, name="diff")
                 nc.vector.tensor_tensor(diff[:], carried[c][:].indirect(listed(h)), silus[c][h][:], ALU.subtract)
                 diffs.append(diff)
-            if late_next:
-                quantise_wh(c + 1, both_passes)
-            if c + 1 < CHUNKS:
-                silus[c + 1] = transform(c + 1)
-            gated = []
+            halves = []
             for h in range(HALVES):
                 twice = ring.tile([P, HALF], F32, name="twice")
-                nc.vector.scalar_tensor_tensor(twice[:], tanhs[h][:], 1.0, diffs[h][:], ALU.add, ALU.mult)
-                gated.append(twice)
+                nc.vector.scalar_tensor_tensor(twice[:], tanhs[c][h][:], 1.0, diffs[h][:], ALU.add, ALU.mult)
+                halves.append(twice)
+            return halves
+
+        def direct_sum(c):
             for h in range(HALVES):
                 pieces = LAST_PIECES if (c, h) == (CHUNKS - 1, HALVES - 1) else 1
                 width = HALF // pieces
                 for k in range(pieces):
                     js = slice(k * width, (k + 1) * width)
                     result = keep.tile([P, width], F32, name=f"result{c}_{h}_{k}")
-                    nc.vector.scalar_tensor_tensor(result[:], gated[h][:, js], 0.5, silus[c][h][:, js], ALU.mult, ALU.add)
+                    nc.vector.scalar_tensor_tensor(result[:], gated[c][h][:, js], 0.5, silus[c][h][:, js], ALU.mult, ALU.add)
                     column = h * HALF + k * width
                     nc.sync.dma_start(out[c * P : (c + 1) * P, column : column + width], result[:])
+
+        silus = {c: transform(c) for c in range(EARLY)}
+        tanhs = {0: gate(0)}
+        gated = {0: blend(0)}
+        direct_sum(0)
+        tanhs[1] = gate(1)
+        round_wh(2)
+        quantise_wh(2, both_passes)
+        tanhs[2] = gate(2)
+        tanhs[3] = gate(3)
+        round_wh(3)
+        silus[2] = transform(2)
+        gated[1] = blend(1)
+        quantise_wh(3, both_passes)
+        sums = [turned_sum(h, gated[1][h], silus[1][h]) for h in range(HALVES)]
+        silus[3] = transform(3)
+        for h in range(HALVES):
+            turn_back(1, h, sums[h])
+        gated[2] = blend(2)
+        sums = [turned_sum(h, gated[2][h], silus[2][h]) for h in range(HALVES)]
+        for h in range(HALVES):
+            turn_back(2, h, sums[h])
+        gated[3] = blend(3)
+        direct_sum(3)

@@ -108,7 +108,7 @@ def tile_list_hwayt_mix_silu_kernel(
         load_wh(early_wh, 0, EARLY)
 
         nc.vector.tensor_copy(picked_scales[:], scale_window[:].bitcast(U8).indirect(offsets[:]))
-        for a, u in ((0, 0), (1, 0), (1, 1), (0, 1)):
+        for a, u in ((1, 0), (1, 1), (0, 0), (0, 1)):
             source = TAIL + SCALE_ROWS * (2 * a + u)
             nc.sync.dma_start(
                 item_planes[a][64 * u : 64 * (u + 1), :], picked_scales[:].bitcast(I32)[source : source + 64, :]
@@ -248,8 +248,8 @@ def tile_list_hwayt_mix_silu_kernel(
                 halves.append(twice)
             return halves
 
-        def direct_sum(c):
-            for h in range(HALVES):
+        def direct_sum(c, halves=range(HALVES)):
+            for h in halves:
                 pieces = LAST_PIECES if (c, h) == (CHUNKS - 1, HALVES - 1) else 1
                 width = HALF // pieces
                 for k in range(pieces):
@@ -277,8 +277,39 @@ def tile_list_hwayt_mix_silu_kernel(
         for h in range(HALVES):
             turn_back(1, h, sums[h])
         gated[2] = blend(2)
-        sums = [turned_sum(h, gated[2][h], silus[2][h]) for h in range(HALVES)]
-        for h in range(HALVES):
-            turn_back(2, h, sums[h])
-        gated[3] = blend(3)
-        direct_sum(3)
+        turn_back(2, 0, turned_sum(0, gated[2][0], silus[2][0]))
+        direct_sum(2, [1])
+        c = CHUNKS - 1
+        pieces = [slice(0, HALF), slice(HALF, HALF + HALF // 2), slice(HALF + HALF // 2, J)]
+        diffs, blends = {}, {}
+
+        def of_piece(halves, js):
+            h = js.start // HALF
+            return halves[h][:, js.start - h * HALF : js.stop - h * HALF]
+
+        def last_diff(n):
+            js = pieces[n]
+            diffs[n] = keep.tile([P, js.stop - js.start], F32, name=f"last_diff{n}")
+            picks = offsets[:, js.start // GROUP : js.stop // GROUP]
+            nc.vector.tensor_tensor(diffs[n][:], carried[c][:].indirect(picks), of_piece(silus[c], js), ALU.subtract)
+
+        def last_blend(n):
+            js = pieces[n]
+            blends[n] = keep.tile([P, js.stop - js.start], F32, name=f"last_blend{n}")
+            nc.vector.scalar_tensor_tensor(blends[n][:], of_piece(tanhs[c], js), 1.0, diffs[n][:], ALU.add, ALU.mult)
+
+        def last_sum(n):
+            js = pieces[n]
+            result = keep.tile([P, js.stop - js.start], F32, name=f"last_result{n}")
+            nc.vector.scalar_tensor_tensor(result[:], blends[n][:], 0.5, of_piece(silus[c], js), ALU.mult, ALU.add)
+            nc.sync.dma_start(out[c * P : (c + 1) * P, js], result[:])
+
+        last_diff(0)
+        last_diff(1)
+        last_blend(0)
+        last_diff(2)
+        last_sum(0)
+        last_blend(1)
+        last_blend(2)
+        last_sum(1)
+        last_sum(2)

@@ -118,12 +118,12 @@ def tile_list_hwayt_mix_silu_kernel(
         load_plane(wg4_plane, wg4_scales)
         nc.sync.dma_start(wg4_codes[:], wg4_words[0].bitcast(I32))
         nc.sync.dma_start(wg8_codes[:], wg8_words[0].rearrange("p n b -> p (n b)").bitcast(I32))
-        load_carried(1, slice(0, T // 2))
+        load_carried(1, slice(0, T // 4))
         for c in range(1, CHUNKS):
             if c + 1 < CHUNKS:
                 late_wh = [keep.tile([P, PACK, P], F32, name=f"late_wh{c + 1}_{a}") for a in range(PASSES)]
                 load_wh(late_wh, c + 1, 1)
-            load_carried(c, slice(T // 2 if c == 1 else 0, T))
+            load_carried(c, slice(T // 4 if c == 1 else 0, T))
 
         grouped = {}
         wh_codes = {}
@@ -263,13 +263,13 @@ def tile_list_hwayt_mix_silu_kernel(
         tanhs = {0: gate(0)}
         gated = {0: blend(0)}
         direct_sum(0)
-        tanhs[1] = gate(1)
         round_wh(2)
         quantise_wh(2, both_passes)
+        tanhs[1] = gate(1)
         tanhs[2] = gate(2)
-        tanhs[3] = gate(3)
-        round_wh(3)
         silus[2] = transform(2)
+        round_wh(3)
+        tanhs[3] = gate(3)
         gated[1] = blend(1)
         quantise_wh(3, both_passes)
         sums = [turned_sum(h, gated[1][h], silus[1][h]) for h in range(HALVES)]

@@ -106,9 +106,10 @@ def tile_list_hwayt_mix_silu_kernel(
             for a in range(PASSES)
         ]
         load_wh(early_wh, 0, EARLY)
+        nc.sync.dma_start(wg4_codes[:], wg4_words[0].bitcast(I32))
 
         nc.vector.tensor_copy(picked_scales[:], scale_window[:].bitcast(U8).indirect(offsets[:]))
-        for a, u in ((1, 0), (1, 1), (0, 0), (0, 1)):
+        for a, u in ((0, 0), (0, 1), (1, 0), (1, 1)):
             source = TAIL + SCALE_ROWS * (2 * a + u)
             nc.sync.dma_start(
                 item_planes[a][64 * u : 64 * (u + 1), :], picked_scales[:].bitcast(I32)[source : source + 64, :]
@@ -116,7 +117,6 @@ def tile_list_hwayt_mix_silu_kernel(
 
         load_carried(0)
         load_plane(wg4_plane, wg4_scales)
-        nc.sync.dma_start(wg4_codes[:], wg4_words[0].bitcast(I32))
         nc.sync.dma_start(wg8_codes[:], wg8_words[0].rearrange("p n b -> p (n b)").bitcast(I32))
         load_carried(1, slice(0, T // 4))
         for c in range(1, CHUNKS):
@@ -170,46 +170,47 @@ def tile_list_hwayt_mix_silu_kernel(
         nc.vector.transpose(bias[:], bias_rows[:])
         nc.scalar.mul(tanh_bias[:], bias[:, 0:QUADRANT:8], -0.5)
 
-        def product(kind, h, weights):
-            acc = psum.tile([P, HALF], F32, name=f"{kind}{h}")
-            for a, (codes, plane) in enumerate(weights):
+        def product(bank, h, weights, order=(0, 1)):
+            acc = psum.tile([P, HALF], F32, name=bank)
+            for a in order:
+                codes, plane = weights[a]
                 nc.tensor.matmul_mx(
                     out=acc[:],
                     lhsT=codes,
                     lhsT_scale=plane,
                     rhs=item_codes[h][:, a, :].bitcast(FP4X4),
                     rhs_scale=item_planes[a][:].bitcast(U8)[:, h * HALF : (h + 1) * HALF],
-                    start=(a == 0),
-                    stop=(a == PASSES - 1),
+                    start=(a == order[0]),
+                    stop=(a == order[-1]),
                 )
             return acc
 
-        def transform(c):
+        def transform_half(c, h, bank, order=(0, 1)):
             weights = [(wh_codes[c][:, a, :].bitcast(FP8X4), wh_plane[c][:, a, :]) for a in range(PASSES)]
-            halves = []
-            for h in range(HALVES):
-                acc = product("back" if c == 1 else "wh_sum", h, weights)
-                silu = keep.tile([P, HALF], F32, name=f"silu{c}_{h}")
-                nc.scalar.activation(silu[:], acc[:], ACT.Silu)
-                halves.append(silu)
-            return halves
+            acc = product(bank, h, weights, order)
+            silu = keep.tile([P, HALF], F32, name=f"silu{c}_{h}")
+            nc.scalar.activation(silu[:], acc[:], ACT.Silu)
+            return silu
 
-        def gate(c):
+        def transform(c):
+            return [transform_half(c, h, f"wh_sum{h}") for h in range(HALVES)]
+
+        def gate_half(c, h, bank):
             cols = slice(c * P, (c + 1) * P)
             weights = [
                 (wg8_codes[:, cols].bitcast(FP8X4), wg8_plane[:].bitcast(U8)[:, cols]),
                 (wg4_codes[:].bitcast(FP4X4)[:, cols], wg4_plane[:].bitcast(U8)[:, cols]),
             ]
-            halves = []
-            for h in range(HALVES):
-                acc = product("turned" if c == 0 else "gate_sum", h, weights)
-                tanh = keep.tile([P, HALF], F32, name=f"tanh{c}_{h}")
-                nc.scalar.activation(tanh[:], acc[:], ACT.Tanh, bias=tanh_bias[:, c : c + 1], scale=-0.5)
-                halves.append(tanh)
-            return halves
+            acc = product(bank, h, weights)
+            tanh = keep.tile([P, HALF], F32, name=f"tanh{c}_{h}")
+            nc.scalar.activation(tanh[:], acc[:], ACT.Tanh, bias=tanh_bias[:, c : c + 1], scale=-0.5)
+            return tanh
 
-        def turned_sum(h, twice, silu):
-            total = psum.tile([P, HALF], F32, name=f"turned{h}")
+        def gate(c):
+            return [gate_half(c, h, f"turned{h}" if c == 0 else f"gate_sum{h}") for h in range(HALVES)]
+
+        def turned_sum(h, twice, silu, kind="turned"):
+            total = psum.tile([P, HALF], F32, name=f"{kind}{h}")
             terms = [silu, silu, twice]
             for n, term in enumerate(terms):
                 for b in range(HALF // P):
@@ -226,14 +227,14 @@ def tile_list_hwayt_mix_silu_kernel(
             nc.scalar.mul(halved[:], total[:], 0.5)
             return halved
 
-        def turn_back(c, h, halved):
+        def turn_back(c, h, halved, queue=nc.sync):
             back = psum.tile([P, HALF], F32, name=f"back{h}")
             for b in range(HALF // P):
                 cols = slice(b * P, (b + 1) * P)
                 nc.tensor.transpose(back[:, cols], halved[:, cols], identity[:])
             result = keep.tile([P, HALF], F32, name=f"result{c}_{h}")
             nc.scalar.copy(result[:], back[:])
-            nc.sync.dma_start(out[c * P : (c + 1) * P, h * HALF : (h + 1) * HALF], result[:])
+            queue.dma_start(out[c * P : (c + 1) * P, h * HALF : (h + 1) * HALF], result[:])
 
         def blend(c):
             diffs = []
@@ -259,8 +260,10 @@ def tile_list_hwayt_mix_silu_kernel(
                     column = h * HALF + k * width
                     nc.sync.dma_start(out[c * P : (c + 1) * P, column : column + width], result[:])
 
-        silus = {c: transform(c) for c in range(EARLY)}
+        silus = {0: [transform_half(0, 0, "wh_sum0"), transform_half(0, 1, "wh_sum1", (1, 0))]}
+        silus[1] = [transform_half(1, 0, "wh_sum0")]
         tanhs = {0: gate(0)}
+        silus[1].append(transform_half(1, 1, "turned0"))
         gated = {0: blend(0)}
         direct_sum(0)
         round_wh(2)
@@ -269,7 +272,6 @@ def tile_list_hwayt_mix_silu_kernel(
         tanhs[2] = gate(2)
         silus[2] = transform(2)
         round_wh(3)
-        tanhs[3] = gate(3)
         gated[1] = blend(1)
         quantise_wh(3, both_passes)
         sums = [turned_sum(h, gated[1][h], silus[1][h]) for h in range(HALVES)]
@@ -277,8 +279,11 @@ def tile_list_hwayt_mix_silu_kernel(
         for h in range(HALVES):
             turn_back(1, h, sums[h])
         gated[2] = blend(2)
-        turn_back(2, 0, turned_sum(0, gated[2][0], silus[2][0]))
-        direct_sum(2, [1])
+        tanhs[3] = [gate_half(3, 0, "wh_sum0")]
+        sums = [turned_sum(h, gated[2][h], silus[2][h], "gate_sum") for h in range(HALVES)]
+        tanhs[3].append(gate_half(3, 1, "wh_sum0"))
+        turn_back(2, 0, sums[0])
+        turn_back(2, 1, sums[1], nc.scalar)
         c = CHUNKS - 1
         pieces = [slice(0, HALF), slice(HALF, HALF + HALF // 2), slice(HALF + HALF // 2, J)]
         diffs, blends = {}, {}

@@ -26,7 +26,7 @@ HALVES = J // HALF
 GROUP = 16
 QUADRANT = 32
 SCALE_ROWS = 4
-TAIL = 16
+SECOND_ROWS = 16
 EARLY = 2
 RUN = 4
 TURNED = (1, 2)
@@ -47,7 +47,8 @@ def tile_list_hwayt_mix_silu_kernel(
         scale_window = keep.tile([P, T // 4], I32, name="scale_window", align_bytes=64)
         word_window = keep.tile([P, T], I32, name="word_window", align_bytes=64)
         picked_scales = keep.tile([P, J], U8, name="picked_scales", align_bytes=64)
-        item_planes = [keep.tile([P, J // 4], I32, name=f"item_plane{a}", align_bytes=64) for a in range(PASSES)]
+        second_plane = keep.tile([P, J // 4], I32, name="second_plane", align_bytes=64)
+        item_planes = [picked_scales[:], second_plane[:].bitcast(U8)]
         wg8_codes = keep.tile([P, N], I32, name="wg8_codes", align_bytes=64)
         wg4_codes = keep.tile([P, N // 2], I32, name="wg4_codes", align_bytes=64)
         wg8_plane = keep.tile([P, N // 4], I32, name="wg8_plane", align_bytes=64)
@@ -58,12 +59,11 @@ def tile_list_hwayt_mix_silu_kernel(
         identity = keep.tile([P, P], F32, name="identity")
         make_identity(nc, identity[:])
 
+        nc.vector.memset(scale_window[:], 0)
         nc.vector.memset(wg8_plane[:], 0)
         nc.vector.memset(bias_rows[:], 0.0)
         nc.vector.memset(wg4_plane[:], 0)
-        nc.vector.memset(scale_window[0:TAIL, :], 0)
-        nc.vector.memset(scale_window[QUADRANT : QUADRANT + TAIL, :], 0)
-        nc.vector.memset(scale_window[2 * QUADRANT : P, :], 0)
+        nc.vector.memset(second_plane[:], 0)
 
         warm = keep.tile([P, 1], F32, name="warm")
         nc.scalar.activation(warm[:], bias_rows[:, 0:1], ACT.Silu)
@@ -91,13 +91,10 @@ def tile_list_hwayt_mix_silu_kernel(
         def listed(h):
             return offsets[:, h * HALF // GROUP : (h + 1) * HALF // GROUP]
 
-        scale_rows = tab_scales.rearrange("a (u x) t -> (a u) x t", u=2).bitcast(I32)
-        for q in range(2):
-            nc.sync.dma_start(
-                scale_window[QUADRANT * q + TAIL : QUADRANT * (q + 1), :],
-                scale_rows[:, SCALE_ROWS * q : SCALE_ROWS * (q + 1), :],
-            )
         nc.sync.dma_start(offsets[:], offs)
+        nc.sync.dma_start(wg4_codes[:], wg4_words[0].bitcast(I32))
+        load_plane(scale_window, tab_scales)
+        nc.sync.dma_start(scale_window[SECOND_ROWS : 2 * SECOND_ROWS, :], tab_scales[1].bitcast(I32))
         nc.sync.dma_start(word_window[:], tab_words[0].rearrange("p t b -> p (t b)").bitcast(I32))
         load_plane(wg8_plane, wg8_scales)
         nc.sync.dma_start(bias_rows[0:P:8, :], bg.rearrange("(c b i) -> b c i", c=CHUNKS, b=P // QUADRANT))
@@ -106,13 +103,13 @@ def tile_list_hwayt_mix_silu_kernel(
             for a in range(PASSES)
         ]
         load_wh(early_wh, 0, EARLY)
-        nc.sync.dma_start(wg4_codes[:], wg4_words[0].bitcast(I32))
 
         nc.vector.tensor_copy(picked_scales[:], scale_window[:].bitcast(U8).indirect(offsets[:]))
-        for a, u in ((0, 0), (0, 1), (1, 0), (1, 1)):
-            source = TAIL + SCALE_ROWS * (2 * a + u)
+        for q in range(P // QUADRANT):
+            source = SECOND_ROWS + SCALE_ROWS * q
             nc.sync.dma_start(
-                item_planes[a][64 * u : 64 * (u + 1), :], picked_scales[:].bitcast(I32)[source : source + 64, :]
+                second_plane[QUADRANT * q : QUADRANT * q + SCALE_ROWS, :],
+                picked_scales[:].bitcast(I32)[source : source + SCALE_ROWS, :],
             )
 
         load_carried(0)
@@ -179,7 +176,7 @@ def tile_list_hwayt_mix_silu_kernel(
                     lhsT=codes,
                     lhsT_scale=plane,
                     rhs=item_codes[h][:, a, :].bitcast(FP4X4),
-                    rhs_scale=item_planes[a][:].bitcast(U8)[:, h * HALF : (h + 1) * HALF],
+                    rhs_scale=item_planes[a][:, h * HALF : (h + 1) * HALF],
                     start=(a == order[0]),
                     stop=(a == order[-1]),
                 )

@@ -55,7 +55,8 @@ def tile_list_hwayt_mix_silu_kernel(
         wg4_plane = keep.tile([P, N // 4], I32, name="wg4_plane", align_bytes=64)
         carried = [keep.tile([P, T], F32, name=f"carried{c}", align_bytes=64) for c in range(CHUNKS)]
         bias_rows = keep.tile([P, QUADRANT], F32, name="bias_rows", align_bytes=64)
-        tanh_bias = keep.tile([P, CHUNKS], F32, name="tanh_bias")
+        scaled_rows = keep.tile([P, QUADRANT], F32, name="scaled_rows", align_bytes=64)
+        tanh_bias = keep.tile([P, QUADRANT], F32, name="tanh_bias", align_bytes=64)
         identity = keep.tile([P, P], F32, name="identity")
         make_identity(nc, identity[:])
 
@@ -92,7 +93,7 @@ def tile_list_hwayt_mix_silu_kernel(
             return offsets[:, h * HALF // GROUP : (h + 1) * HALF // GROUP]
 
         nc.sync.dma_start(offsets[:], offs)
-        nc.sync.dma_start(wg4_codes[:], wg4_words[0].bitcast(I32))
+        nc.sync.dma_start(wg8_codes[:], wg8_words[0].rearrange("p n b -> p (n b)").bitcast(I32))
         load_plane(scale_window, tab_scales)
         nc.sync.dma_start(scale_window[SECOND_ROWS : 2 * SECOND_ROWS, :], tab_scales[1].bitcast(I32))
         nc.sync.dma_start(word_window[:], tab_words[0].rearrange("p t b -> p (t b)").bitcast(I32))
@@ -114,7 +115,7 @@ def tile_list_hwayt_mix_silu_kernel(
 
         load_carried(0)
         load_plane(wg4_plane, wg4_scales)
-        nc.sync.dma_start(wg8_codes[:], wg8_words[0].rearrange("p n b -> p (n b)").bitcast(I32))
+        nc.sync.dma_start(wg4_codes[:], wg4_words[0].bitcast(I32))
         load_carried(1, slice(0, T // 4))
         for c in range(1, CHUNKS):
             if c + 1 < CHUNKS:
@@ -160,12 +161,10 @@ def tile_list_hwayt_mix_silu_kernel(
             nc.vector.tensor_copy(picked_words[h][:].bitcast(U32), word_window[:].bitcast(U32).indirect(listed(h)))
         part_words(0, keep.tile([P, PASSES, HALF], U16, name="parted0", align_bytes=64))
         quantise_wh(0, each_pass)
-        part_words(1, reused.tile([P, PASSES, HALF], U16, name="parted1", offset=early_bytes, align_bytes=64))
+        part_words(1, reused.tile([P, PASSES, HALF], U16, name="parted1", offset=0, align_bytes=64))
         quantise_wh(1, both_passes)
-        parted_bytes = PASSES * HALF * 2
-        bias = reused.tile([P, QUADRANT], F32, name="bias", offset=early_bytes + parted_bytes, align_bytes=64)
-        nc.vector.transpose(bias[:], bias_rows[:])
-        nc.scalar.mul(tanh_bias[:], bias[:, 0:QUADRANT:8], -0.5)
+        nc.scalar.mul(scaled_rows[:], bias_rows[:], -0.5)
+        nc.vector.transpose(tanh_bias[:], scaled_rows[:])
 
         def product(bank, h, weights, order=(0, 1)):
             acc = psum.tile([P, HALF], F32, name=bank)
@@ -198,9 +197,9 @@ def tile_list_hwayt_mix_silu_kernel(
                 (wg8_codes[:, cols].bitcast(FP8X4), wg8_plane[:].bitcast(U8)[:, cols]),
                 (wg4_codes[:].bitcast(FP4X4)[:, cols], wg4_plane[:].bitcast(U8)[:, cols]),
             ]
-            acc = product(bank, h, weights)
+            acc = product(bank, h, weights, (1, 0))
             tanh = keep.tile([P, HALF], F32, name=f"tanh{c}_{h}")
-            nc.scalar.activation(tanh[:], acc[:], ACT.Tanh, bias=tanh_bias[:, c : c + 1], scale=-0.5)
+            nc.scalar.activation(tanh[:], acc[:], ACT.Tanh, bias=tanh_bias[:, 8 * c : 8 * c + 1], scale=-0.5)
             return tanh
 
         def gate(c):

@@ -49,7 +49,7 @@ def tile_list_hwayt_mix_silu_kernel(
         picked_scales = keep.tile([P, J], U8, name="picked_scales", align_bytes=64)
         second_plane = keep.tile([P, J // 4], I32, name="second_plane", align_bytes=64)
         item_planes = [picked_scales[:], second_plane[:].bitcast(U8)]
-        wg8_codes = keep.tile([P, N], I32, name="wg8_codes", align_bytes=64)
+        wg8_codes = [keep.tile([P, N // 2], I32, name=f"wg8_codes{g}", align_bytes=64) for g in range(2)]
         wg4_codes = keep.tile([P, N // 2], I32, name="wg4_codes", align_bytes=64)
         wg8_plane = keep.tile([P, N // 4], I32, name="wg8_plane", align_bytes=64)
         wg4_plane = keep.tile([P, N // 4], I32, name="wg4_plane", align_bytes=64)
@@ -70,21 +70,18 @@ def tile_list_hwayt_mix_silu_kernel(
         nc.scalar.activation(warm[:], bias_rows[:, 0:1], ACT.Silu)
 
         def load_plane(plane, scales):
-            rows = scales[0].bitcast(I32)
-            for q in range(P // QUADRANT):
-                nc.sync.dma_start(
-                    plane[QUADRANT * q : QUADRANT * q + SCALE_ROWS, :], rows[SCALE_ROWS * q : SCALE_ROWS * (q + 1), :]
-                )
+            rows = scales[0].bitcast(I32).rearrange("(q r) n -> r q n", r=SCALE_ROWS)
+            for r in range(SCALE_ROWS):
+                nc.sync.dma_start(plane[r:P:QUADRANT, :], rows[r])
 
         wh_rows = wh.rearrange("(a p i) n -> a p i n", a=PASSES, i=PACK)
         wh_raw = {}
         early_bytes = PACK * EARLY * P * 4
 
-        def load_wh(tiles, first, count):
-            for a in range(PASSES):
-                nc.sync.dma_start(tiles[a][:], wh_rows[a][:, :, first * P : (first + count) * P])
-                for k in range(count):
-                    wh_raw[first + k, a] = tiles[a][:, :, k * P : (k + 1) * P]
+        def load_wh(tile, first, a):
+            nc.sync.dma_start(tile, wh_rows[a][:, :, first * P : (first + EARLY) * P])
+            for k in range(EARLY):
+                wh_raw[first + k, a] = tile[:, :, k * P : (k + 1) * P]
 
         def load_carried(c, cols=slice(0, T)):
             nc.sync.dma_start(carried[c][:, cols], rT[c * P : (c + 1) * P, cols])
@@ -93,7 +90,8 @@ def tile_list_hwayt_mix_silu_kernel(
             return offsets[:, h * HALF // GROUP : (h + 1) * HALF // GROUP]
 
         nc.sync.dma_start(offsets[:], offs)
-        nc.sync.dma_start(wg8_codes[:], wg8_words[0].rearrange("p n b -> p (n b)").bitcast(I32))
+        wg8_rows = wg8_words[0].rearrange("p n b -> p (n b)").bitcast(I32)
+        nc.sync.dma_start(wg8_codes[0][:], wg8_rows[:, 0 : N // 2])
         load_plane(scale_window, tab_scales)
         nc.sync.dma_start(scale_window[SECOND_ROWS : 2 * SECOND_ROWS, :], tab_scales[1].bitcast(I32))
         nc.sync.dma_start(word_window[:], tab_words[0].rearrange("p t b -> p (t b)").bitcast(I32))
@@ -103,41 +101,46 @@ def tile_list_hwayt_mix_silu_kernel(
             reused.tile([P, PACK, EARLY * P], F32, name=f"early_wh{a}", offset=a * early_bytes, align_bytes=64)
             for a in range(PASSES)
         ]
-        load_wh(early_wh, 0, EARLY)
+        for a in range(PASSES):
+            load_wh(early_wh[a][:], 0, a)
 
         nc.vector.tensor_copy(picked_scales[:], scale_window[:].bitcast(U8).indirect(offsets[:]))
-        for q in range(P // QUADRANT):
-            source = SECOND_ROWS + SCALE_ROWS * q
+        for r in range(SCALE_ROWS):
             nc.sync.dma_start(
-                second_plane[QUADRANT * q : QUADRANT * q + SCALE_ROWS, :],
-                picked_scales[:].bitcast(I32)[source : source + SCALE_ROWS, :],
+                second_plane[r:P:QUADRANT, :],
+                picked_scales[:].bitcast(I32)[SECOND_ROWS + r : 2 * SECOND_ROWS : SCALE_ROWS, :],
             )
 
         load_carried(0)
         load_plane(wg4_plane, wg4_scales)
         nc.sync.dma_start(wg4_codes[:], wg4_words[0].bitcast(I32))
-        load_carried(1, slice(0, T // 4))
-        for c in range(1, CHUNKS):
-            if c + 1 < CHUNKS:
-                late_wh = [keep.tile([P, PACK, P], F32, name=f"late_wh{c + 1}_{a}") for a in range(PASSES)]
-                load_wh(late_wh, c + 1, 1)
-            load_carried(c, slice(T // 4 if c == 1 else 0, T))
+        late_first = keep.tile([P, PACK, EARLY * P], F32, name="late_first")
+        load_wh(late_first[:], EARLY, 0)
+        nc.sync.dma_start(wg8_codes[1][:], wg8_rows[:, N // 2 : N])
+        load_carried(1)
+        late_offset = PASSES * early_bytes
+        late_second = reused.tile([P, 6, EARLY * P], F32, name="late_second", offset=late_offset, align_bytes=64)
+        load_wh(late_second[:, 0:PACK, :], EARLY, 1)
+        load_carried(2)
+        load_carried(3)
 
         grouped = {}
         wh_codes = {}
         wh_plane = {}
 
-        def round_wh(c):
+        for c in range(CHUNKS):
             grouped[c] = keep.tile([P, PASSES, P, PACK], BF16, name=f"grouped{c}", align_bytes=64)
-            for a in range(PASSES):
+            wh_codes[c] = keep.tile([P, PASSES, P], U32, name=f"wh_codes{c}", align_bytes=64)
+            wh_plane[c] = keep.tile([P, PASSES, P], U8, name=f"wh_plane{c}", align_bytes=64)
+
+        def round_wh(c, passes=range(PASSES)):
+            for a in passes:
                 nc.scalar.copy(
                     grouped[c][:, a].rearrange("p (m v) i -> p m i v", v=RUN),
                     wh_raw[c, a].rearrange("p i (m v) -> p m i v", v=RUN),
                 )
 
         def quantise_wh(c, calls):
-            wh_codes[c] = keep.tile([P, PASSES, P], U32, name=f"wh_codes{c}", align_bytes=64)
-            wh_plane[c] = keep.tile([P, PASSES, P], U8, name=f"wh_plane{c}", align_bytes=64)
             for passes in calls:
                 nc.vector.quantize_mx(
                     out=wh_codes[c][:, passes].rearrange("p a n -> p (a n)").bitcast(FP8X4),
@@ -188,25 +191,21 @@ def tile_list_hwayt_mix_silu_kernel(
             nc.scalar.activation(silu[:], acc[:], ACT.Silu)
             return silu
 
-        def transform(c):
-            return [transform_half(c, h, f"wh_sum{h}") for h in range(HALVES)]
-
-        def gate_half(c, h, bank):
+        def gate_half(c, h, bank, order=(1, 0), tanh=None):
             cols = slice(c * P, (c + 1) * P)
+            own = slice(c % 2 * P, (c % 2 + 1) * P)
             weights = [
-                (wg8_codes[:, cols].bitcast(FP8X4), wg8_plane[:].bitcast(U8)[:, cols]),
+                (wg8_codes[c // 2][:, own].bitcast(FP8X4), wg8_plane[:].bitcast(U8)[:, cols]),
                 (wg4_codes[:].bitcast(FP4X4)[:, cols], wg4_plane[:].bitcast(U8)[:, cols]),
             ]
-            acc = product(bank, h, weights, (1, 0))
-            tanh = keep.tile([P, HALF], F32, name=f"tanh{c}_{h}")
+            acc = product(bank, h, weights, order)
+            if tanh is None:
+                tanh = keep.tile([P, HALF], F32, name=f"tanh{c}_{h}")
             nc.scalar.activation(tanh[:], acc[:], ACT.Tanh, bias=tanh_bias[:, 8 * c : 8 * c + 1], scale=-0.5)
             return tanh
 
-        def gate(c):
-            return [gate_half(c, h, f"turned{h}" if c == 0 else f"gate_sum{h}") for h in range(HALVES)]
-
-        def turned_sum(h, twice, silu, kind="turned"):
-            total = psum.tile([P, HALF], F32, name=f"{kind}{h}")
+        def turned_sum(twice, silu, bank):
+            total = psum.tile([P, HALF], F32, name=bank)
             terms = [silu, silu, twice]
             for n, term in enumerate(terms):
                 for b in range(HALF // P):
@@ -223,8 +222,8 @@ def tile_list_hwayt_mix_silu_kernel(
             nc.scalar.mul(halved[:], total[:], 0.5)
             return halved
 
-        def turn_back(c, h, halved, queue=nc.sync):
-            back = psum.tile([P, HALF], F32, name=f"back{h}")
+        def turn_back(c, h, halved, bank, queue=nc.sync):
+            back = psum.tile([P, HALF], F32, name=bank)
             for b in range(HALF // P):
                 cols = slice(b * P, (b + 1) * P)
                 nc.tensor.transpose(back[:, cols], halved[:, cols], identity[:])
@@ -232,7 +231,7 @@ def tile_list_hwayt_mix_silu_kernel(
             nc.scalar.copy(result[:], back[:])
             queue.dma_start(out[c * P : (c + 1) * P, h * HALF : (h + 1) * HALF], result[:])
 
-        def blend(c):
+        def blend(c, into=None):
             diffs = []
             for h in range(HALVES):
                 diff = ring.tile([P, HALF], F32, name="diff")
@@ -240,7 +239,7 @@ def tile_list_hwayt_mix_silu_kernel(
                 diffs.append(diff)
             halves = []
             for h in range(HALVES):
-                twice = ring.tile([P, HALF], F32, name="twice")
+                twice = ring.tile([P, HALF], F32, name="twice") if into is None else into[h]
                 nc.vector.scalar_tensor_tensor(twice[:], tanhs[c][h][:], 1.0, diffs[h][:], ALU.add, ALU.mult)
                 halves.append(twice)
             return halves
@@ -256,30 +255,39 @@ def tile_list_hwayt_mix_silu_kernel(
                     column = h * HALF + k * width
                     nc.sync.dma_start(out[c * P : (c + 1) * P, column : column + width], result[:])
 
-        silus = {0: [transform_half(0, 0, "wh_sum0"), transform_half(0, 1, "wh_sum1", (1, 0))]}
-        silus[1] = [transform_half(1, 0, "wh_sum0")]
-        tanhs = {0: gate(0)}
-        silus[1].append(transform_half(1, 1, "turned0"))
+        def after_rounding(n, name):
+            return reused.tile([P, HALF], F32, name=name, offset=late_offset + n * HALF * 4, align_bytes=64)
+
+        silus = {0: [transform_half(0, 0, "bank_a"), transform_half(0, 1, "bank_b", (1, 0))]}
+        silus[1] = [transform_half(1, 0, "bank_a")]
+        tanhs = {0: [gate_half(0, 0, "bank_c", (0, 1)), gate_half(0, 1, "bank_d")]}
+        silus[1].append(transform_half(1, 1, "bank_c"))
         gated = {0: blend(0)}
         direct_sum(0)
-        round_wh(2)
-        quantise_wh(2, both_passes)
-        tanhs[1] = gate(1)
-        tanhs[2] = gate(2)
-        silus[2] = transform(2)
-        round_wh(3)
-        gated[1] = blend(1)
-        quantise_wh(3, both_passes)
-        sums = [turned_sum(h, gated[1][h], silus[1][h]) for h in range(HALVES)]
-        silus[3] = transform(3)
-        for h in range(HALVES):
-            turn_back(1, h, sums[h])
+        for c in (2, 3):
+            round_wh(c, [0])
+            quantise_wh(c, each_pass[:1])
+        tanhs[1] = [gate_half(1, 0, "bank_d"), gate_half(1, 1, "bank_c")]
+        tanhs[2] = [gate_half(2, 0, "bank_e", (0, 1))]
+        for c in (2, 3):
+            round_wh(c, [1])
+            quantise_wh(c, each_pass[1:])
+        tanhs[2].append(gate_half(2, 1, "bank_e", tanh=after_rounding(2, "tanh2_1")))
+        silus[2] = [transform_half(2, 0, "bank_a"), transform_half(2, 1, "bank_b")]
+        gated[1] = blend(1, [after_rounding(h, f"twice1_{h}") for h in range(HALVES)])
+        first_sum = turned_sum(gated[1][0], silus[1][0], "bank_d")
+        silus[3] = [transform_half(3, 0, "bank_e")]
+        second_sum = turned_sum(gated[1][1], silus[1][1], "bank_c")
+        turn_back(1, 0, first_sum, "bank_f")
+        silus[3].append(transform_half(3, 1, "bank_e"))
+        turn_back(1, 1, second_sum, "bank_g")
         gated[2] = blend(2)
-        tanhs[3] = [gate_half(3, 0, "wh_sum0")]
-        sums = [turned_sum(h, gated[2][h], silus[2][h], "gate_sum") for h in range(HALVES)]
-        tanhs[3].append(gate_half(3, 1, "wh_sum0"))
-        turn_back(2, 0, sums[0])
-        turn_back(2, 1, sums[1], nc.scalar)
+        first_sum = turned_sum(gated[2][0], silus[2][0], "bank_a")
+        tanhs[3] = [gate_half(3, 0, "bank_e")]
+        second_sum = turned_sum(gated[2][1], silus[2][1], "bank_b")
+        tanhs[3].append(gate_half(3, 1, "bank_e"))
+        turn_back(2, 0, first_sum, "bank_h")
+        turn_back(2, 1, second_sum, "bank_d", nc.scalar)
         c = CHUNKS - 1
         pieces = [slice(0, HALF), slice(HALF, HALF + HALF // 2), slice(HALF + HALF // 2, J)]
         diffs, blends = {}, {}

@@ -86,9 +86,6 @@ def tile_list_hwayt_mix_silu_kernel(
         def load_carried(c, cols=slice(0, T)):
             nc.sync.dma_start(carried[c][:, cols], rT[c * P : (c + 1) * P, cols])
 
-        def listed(h):
-            return offsets[:, h * HALF // GROUP : (h + 1) * HALF // GROUP]
-
         nc.sync.dma_start(offsets[:], offs)
         wg8_rows = wg8_words[0].rearrange("p n b -> p (n b)").bitcast(I32)
         nc.sync.dma_start(wg8_codes[0][:], wg8_rows[:, 0 : N // 2])
@@ -151,44 +148,61 @@ def tile_list_hwayt_mix_silu_kernel(
         each_pass = [slice(a, a + 1) for a in range(PASSES)]
         both_passes = [slice(0, PASSES)]
 
-        picked_words = [keep.tile([P, HALF], I32, name=f"picked_words{h}", align_bytes=64) for h in range(HALVES)]
         item_codes = []
 
-        def part_words(h, parted):
-            nc.vector.tensor_copy(parted[:], picked_words[h][:].bitcast(U16).rearrange("p (j a) -> p a j", a=PASSES))
+        picked_words = {}
+        picked_offset = late_offset + 6 * EARLY * P * 4
+
+        def pick_words(h, js, place):
+            picked = reused.tile(
+                [P, js.stop - js.start], I32, name=f"picked{h}_{js.start}", offset=picked_offset + place, align_bytes=64
+            )
+            picks = offsets[:, (h * HALF + js.start) // GROUP : (h * HALF + js.stop) // GROUP]
+            nc.vector.tensor_copy(picked[:].bitcast(U32), word_window[:].bitcast(U32).indirect(picks))
+            picked_words[h, js.start] = picked
+
+        def part_words(h, parted, pieces):
+            for js in pieces:
+                nc.vector.tensor_copy(
+                    parted[:, :, js], picked_words[h, js.start][:].bitcast(U16).rearrange("p (j a) -> p a j", a=PASSES)
+                )
             item_codes.append(parted)
+
+        whole = [slice(0, HALF)]
+        quarters = [slice(0, HALF // 2), slice(HALF // 2, HALF)]
 
         for c in range(EARLY):
             round_wh(c)
-        for h in range(HALVES):
-            nc.vector.tensor_copy(picked_words[h][:].bitcast(U32), word_window[:].bitcast(U32).indirect(listed(h)))
-        part_words(0, keep.tile([P, PASSES, HALF], U16, name="parted0", align_bytes=64))
+        pick_words(0, quarters[0], 0)
+        pick_words(0, quarters[1], HALF * 4)
+        part_words(0, keep.tile([P, PASSES, HALF], U16, name="parted0", align_bytes=64), quarters)
+        pick_words(1, whole[0], 0)
         quantise_wh(0, each_pass)
-        part_words(1, reused.tile([P, PASSES, HALF], U16, name="parted1", offset=0, align_bytes=64))
+        part_words(1, reused.tile([P, PASSES, HALF], U16, name="parted1", offset=0, align_bytes=64), whole)
         quantise_wh(1, both_passes)
         nc.scalar.mul(scaled_rows[:], bias_rows[:], -0.5)
         nc.vector.transpose(tanh_bias[:], scaled_rows[:])
 
-        def product(bank, h, weights, order=(0, 1)):
-            acc = psum.tile([P, HALF], F32, name=bank)
+        def product(bank, h, weights, order=(0, 1), js=slice(0, HALF)):
+            acc = psum.tile([P, HALF], F32, name=bank)[:, 0 : js.stop - js.start]
             for a in order:
                 codes, plane = weights[a]
                 nc.tensor.matmul_mx(
-                    out=acc[:],
+                    out=acc,
                     lhsT=codes,
                     lhsT_scale=plane,
-                    rhs=item_codes[h][:, a, :].bitcast(FP4X4),
-                    rhs_scale=item_planes[a][:, h * HALF : (h + 1) * HALF],
+                    rhs=item_codes[h][:, a, js].bitcast(FP4X4),
+                    rhs_scale=item_planes[a][:, h * HALF + js.start : h * HALF + js.stop],
                     start=(a == order[0]),
                     stop=(a == order[-1]),
                 )
             return acc
 
-        def transform_half(c, h, bank, order=(0, 1)):
+        def transform_half(c, h, banks, order=(0, 1)):
             weights = [(wh_codes[c][:, a, :].bitcast(FP8X4), wh_plane[c][:, a, :]) for a in range(PASSES)]
-            acc = product(bank, h, weights, order)
             silu = keep.tile([P, HALF], F32, name=f"silu{c}_{h}")
-            nc.scalar.activation(silu[:], acc[:], ACT.Silu)
+            for bank, js in zip(banks, whole if len(banks) == 1 else quarters):
+                nc.scalar.activation(silu[:, js], product(bank, h, weights, order, js), ACT.Silu)
             return silu
 
         def gate_half(c, h, bank, order=(1, 0), tanh=None):
@@ -201,7 +215,7 @@ def tile_list_hwayt_mix_silu_kernel(
             acc = product(bank, h, weights, order)
             if tanh is None:
                 tanh = keep.tile([P, HALF], F32, name=f"tanh{c}_{h}")
-            nc.scalar.activation(tanh[:], acc[:], ACT.Tanh, bias=tanh_bias[:, 8 * c : 8 * c + 1], scale=-0.5)
+            nc.scalar.activation(tanh[:], acc, ACT.Tanh, bias=tanh_bias[:, 8 * c : 8 * c + 1], scale=-0.5)
             return tanh
 
         def turned_sum(twice, silu, bank):
@@ -231,11 +245,13 @@ def tile_list_hwayt_mix_silu_kernel(
             nc.scalar.copy(result[:], back[:])
             queue.dma_start(out[c * P : (c + 1) * P, h * HALF : (h + 1) * HALF], result[:])
 
-        def blend(c, into=None):
+        def blend(c, into=None, first=whole):
             diffs = []
             for h in range(HALVES):
                 diff = ring.tile([P, HALF], F32, name="diff")
-                nc.vector.tensor_tensor(diff[:], carried[c][:].indirect(listed(h)), silus[c][h][:], ALU.subtract)
+                for js in first if h == 0 else whole:
+                    picks = offsets[:, (h * HALF + js.start) // GROUP : (h * HALF + js.stop) // GROUP]
+                    nc.vector.tensor_tensor(diff[:, js], carried[c][:].indirect(picks), silus[c][h][:, js], ALU.subtract)
                 diffs.append(diff)
             halves = []
             for h in range(HALVES):
@@ -258,32 +274,32 @@ def tile_list_hwayt_mix_silu_kernel(
         def after_rounding(n, name):
             return reused.tile([P, HALF], F32, name=name, offset=late_offset + n * HALF * 4, align_bytes=64)
 
-        silus = {0: [transform_half(0, 0, "bank_a"), transform_half(0, 1, "bank_b", (1, 0))]}
-        silus[1] = [transform_half(1, 0, "bank_a")]
-        tanhs = {0: [gate_half(0, 0, "bank_c", (0, 1)), gate_half(0, 1, "bank_d")]}
-        silus[1].append(transform_half(1, 1, "bank_c"))
-        gated = {0: blend(0)}
+        silus = {0: [transform_half(0, 0, ["bank_h", "bank_a"]), transform_half(0, 1, ["bank_b"], (1, 0))]}
+        silus[1] = [transform_half(1, 0, ["bank_a"])]
+        tanhs = {0: [gate_half(0, 0, "bank_c", (0, 1)), gate_half(0, 1, "bank_d", (0, 1))]}
+        silus[1].append(transform_half(1, 1, ["bank_c"]))
+        gated = {0: blend(0, first=quarters)}
         direct_sum(0)
         for c in (2, 3):
             round_wh(c, [0])
             quantise_wh(c, each_pass[:1])
-        tanhs[1] = [gate_half(1, 0, "bank_d"), gate_half(1, 1, "bank_c")]
+        tanhs[1] = [gate_half(1, 0, "bank_f", (0, 1)), gate_half(1, 1, "bank_c")]
         tanhs[2] = [gate_half(2, 0, "bank_e", (0, 1))]
         for c in (2, 3):
             round_wh(c, [1])
             quantise_wh(c, each_pass[1:])
         tanhs[2].append(gate_half(2, 1, "bank_e", tanh=after_rounding(2, "tanh2_1")))
-        silus[2] = [transform_half(2, 0, "bank_a"), transform_half(2, 1, "bank_b")]
+        silus[2] = [transform_half(2, 0, ["bank_a", "bank_g"]), transform_half(2, 1, ["bank_b"])]
         gated[1] = blend(1, [after_rounding(h, f"twice1_{h}") for h in range(HALVES)])
         first_sum = turned_sum(gated[1][0], silus[1][0], "bank_d")
-        silus[3] = [transform_half(3, 0, "bank_e")]
+        silus[3] = [transform_half(3, 0, ["bank_e"])]
         second_sum = turned_sum(gated[1][1], silus[1][1], "bank_c")
         turn_back(1, 0, first_sum, "bank_f")
-        silus[3].append(transform_half(3, 1, "bank_e"))
+        silus[3].append(transform_half(3, 1, ["bank_e"]))
         turn_back(1, 1, second_sum, "bank_g")
-        gated[2] = blend(2)
+        gated[2] = blend(2, first=quarters)
         first_sum = turned_sum(gated[2][0], silus[2][0], "bank_a")
-        tanhs[3] = [gate_half(3, 0, "bank_e")]
+        tanhs[3] = [gate_half(3, 0, "bank_f")]
         second_sum = turned_sum(gated[2][1], silus[2][1], "bank_b")
         tanhs[3].append(gate_half(3, 1, "bank_e"))
         turn_back(2, 0, first_sum, "bank_h")

@@ -178,7 +178,7 @@ def tile_list_hwayt_mix_silu_kernel(
         part_words(0, keep.tile([P, PASSES, HALF], U16, name="parted0", align_bytes=64), quarters)
         pick_words(1, whole[0], 0)
         quantise_wh(0, each_pass)
-        part_words(1, reused.tile([P, PASSES, HALF], U16, name="parted1", offset=0, align_bytes=64), whole)
+        part_words(1, reused.tile([P, PASSES, HALF], U16, name="parted1", offset=early_bytes, align_bytes=64), whole)
         quantise_wh(1, both_passes)
         nc.scalar.mul(scaled_rows[:], bias_rows[:], -0.5)
         nc.vector.transpose(tanh_bias[:], scaled_rows[:])
@@ -276,7 +276,7 @@ def tile_list_hwayt_mix_silu_kernel(
 
         silus = {0: [transform_half(0, 0, ["bank_h", "bank_a"]), transform_half(0, 1, ["bank_b"], (1, 0))]}
         silus[1] = [transform_half(1, 0, ["bank_a"])]
-        tanhs = {0: [gate_half(0, 0, "bank_c", (0, 1)), gate_half(0, 1, "bank_d", (0, 1))]}
+        tanhs = {0: [gate_half(0, 0, "bank_c", (0, 1)), gate_half(0, 1, "bank_h", (0, 1))]}
         silus[1].append(transform_half(1, 1, ["bank_c"]))
         gated = {0: blend(0, first=quarters)}
         direct_sum(0)
@@ -291,7 +291,7 @@ def tile_list_hwayt_mix_silu_kernel(
         tanhs[2].append(gate_half(2, 1, "bank_e", tanh=after_rounding(2, "tanh2_1")))
         silus[2] = [transform_half(2, 0, ["bank_a", "bank_g"]), transform_half(2, 1, ["bank_b"])]
         gated[1] = blend(1, [after_rounding(h, f"twice1_{h}") for h in range(HALVES)])
-        first_sum = turned_sum(gated[1][0], silus[1][0], "bank_d")
+        first_sum = turned_sum(gated[1][0], silus[1][0], "bank_h")
         silus[3] = [transform_half(3, 0, ["bank_e"])]
         second_sum = turned_sum(gated[1][1], silus[1][1], "bank_c")
         turn_back(1, 0, first_sum, "bank_f")
@@ -300,10 +300,8 @@ def tile_list_hwayt_mix_silu_kernel(
         gated[2] = blend(2, first=quarters)
         first_sum = turned_sum(gated[2][0], silus[2][0], "bank_a")
         tanhs[3] = [gate_half(3, 0, "bank_f")]
-        second_sum = turned_sum(gated[2][1], silus[2][1], "bank_b")
         tanhs[3].append(gate_half(3, 1, "bank_e"))
-        turn_back(2, 0, first_sum, "bank_h")
-        turn_back(2, 1, second_sum, "bank_d", nc.scalar)
+        turn_back(2, 0, first_sum, "bank_d", nc.scalar)
         c = CHUNKS - 1
         pieces = [slice(0, HALF), slice(HALF, HALF + HALF // 2), slice(HALF + HALF // 2, J)]
         diffs, blends = {}, {}
@@ -330,6 +328,7 @@ def tile_list_hwayt_mix_silu_kernel(
             nc.sync.dma_start(out[c * P : (c + 1) * P, js], result[:])
 
         last_diff(0)
+        direct_sum(2, [1])
         last_diff(1)
         last_blend(0)
         last_diff(2)

@@ -89,8 +89,9 @@ def tile_list_hwayt_mix_silu_kernel(
         nc.sync.dma_start(offsets[:], offs)
         wg8_rows = wg8_words[0].rearrange("p n b -> p (n b)").bitcast(I32)
         nc.sync.dma_start(wg8_codes[0][:], wg8_rows[:, 0 : N // 2])
-        load_plane(scale_window, tab_scales)
-        nc.sync.dma_start(scale_window[SECOND_ROWS : 2 * SECOND_ROWS, :], tab_scales[1].bitcast(I32))
+        table_rows = tab_scales.bitcast(I32).rearrange("a (q r) t -> r q a t", r=SCALE_ROWS)
+        for r in range(SCALE_ROWS):
+            nc.sync.dma_start(scale_window[r:P:SECOND_ROWS, :], table_rows[r])
         nc.sync.dma_start(word_window[:], tab_words[0].rearrange("p t b -> p (t b)").bitcast(I32))
         load_plane(wg8_plane, wg8_scales)
         nc.sync.dma_start(bias_rows[0:P:8, :], bg.rearrange("(c b i) -> b c i", c=CHUNKS, b=P // QUADRANT))
@@ -105,7 +106,7 @@ def tile_list_hwayt_mix_silu_kernel(
         for r in range(SCALE_ROWS):
             nc.sync.dma_start(
                 second_plane[r:P:QUADRANT, :],
-                picked_scales[:].bitcast(I32)[SECOND_ROWS + r : 2 * SECOND_ROWS : SCALE_ROWS, :],
+                picked_scales[:].bitcast(I32)[SECOND_ROWS + r : P : QUADRANT, :],
             )
 
         load_carried(0)
@@ -155,7 +156,7 @@ def tile_list_hwayt_mix_silu_kernel(
 
         def pick_words(h, js, place):
             picked = reused.tile(
-                [P, js.stop - js.start], I32, name=f"picked{h}_{js.start}", offset=picked_offset + place, align_bytes=64
+                [P, js.stop - js.start], I32, name=f"picked{h}_{js.start}", offset=place, align_bytes=64
             )
             picks = offsets[:, (h * HALF + js.start) // GROUP : (h * HALF + js.stop) // GROUP]
             nc.vector.tensor_copy(picked[:].bitcast(U32), word_window[:].bitcast(U32).indirect(picks))
@@ -173,12 +174,14 @@ def tile_list_hwayt_mix_silu_kernel(
 
         for c in range(EARLY):
             round_wh(c)
-        pick_words(0, quarters[0], 0)
-        pick_words(0, quarters[1], HALF * 4)
+        pick_words(0, quarters[0], picked_offset)
+        pick_words(0, quarters[1], picked_offset + HALF * 2)
         part_words(0, keep.tile([P, PASSES, HALF], U16, name="parted0", align_bytes=64), quarters)
-        pick_words(1, whole[0], 0)
-        quantise_wh(0, each_pass)
-        part_words(1, reused.tile([P, PASSES, HALF], U16, name="parted1", offset=early_bytes, align_bytes=64), whole)
+        pick_words(1, quarters[0], picked_offset)
+        quantise_wh(0, each_pass[:1])
+        pick_words(1, quarters[1], 0)
+        quantise_wh(0, each_pass[1:])
+        part_words(1, reused.tile([P, PASSES, HALF], U16, name="parted1", offset=early_bytes, align_bytes=64), quarters)
         quantise_wh(1, both_passes)
         nc.scalar.mul(scaled_rows[:], bias_rows[:], -0.5)
         nc.vector.transpose(tanh_bias[:], scaled_rows[:])

@@ -221,11 +221,12 @@ def tile_list_hwayt_mix_silu_kernel(
             nc.scalar.activation(tanh[:], acc, ACT.Tanh, bias=tanh_bias[:, 8 * c : 8 * c + 1], scale=-0.5)
             return tanh
 
-        def turned_sum(twice, silu, bank):
+        def turned_sum(twice, silu, bank, blend_first=False):
             total = psum.tile([P, HALF], F32, name=bank)
-            terms = [silu, silu, twice]
+            width = twice.shape[1]
+            terms = [twice, silu, silu] if blend_first else [silu, silu, twice]
             for n, term in enumerate(terms):
-                for b in range(HALF // P):
+                for b in range(width // P):
                     cols = slice(b * P, (b + 1) * P)
                     nc.tensor.matmul(
                         total[:, cols],
@@ -233,20 +234,21 @@ def tile_list_hwayt_mix_silu_kernel(
                         rhs=identity[:],
                         is_transpose=True,
                         start=(n == 0 and b == 0),
-                        stop=(n == len(terms) - 1 and b == HALF // P - 1),
+                        stop=(n == len(terms) - 1 and b == width // P - 1),
                     )
             halved = ring.tile([P, HALF], F32, name="halved")
-            nc.scalar.mul(halved[:], total[:], 0.5)
-            return halved
+            nc.scalar.mul(halved[:, 0:width], total[:, 0:width], 0.5)
+            return halved[:, 0:width]
 
         def turn_back(c, h, halved, bank, queue=nc.sync):
+            width = halved.shape[1]
             back = psum.tile([P, HALF], F32, name=bank)
-            for b in range(HALF // P):
+            for b in range(width // P):
                 cols = slice(b * P, (b + 1) * P)
                 nc.tensor.transpose(back[:, cols], halved[:, cols], identity[:])
-            result = keep.tile([P, HALF], F32, name=f"result{c}_{h}")
-            nc.scalar.copy(result[:], back[:])
-            queue.dma_start(out[c * P : (c + 1) * P, h * HALF : (h + 1) * HALF], result[:])
+            result = keep.tile([P, width], F32, name=f"result{c}_{h}")
+            nc.scalar.copy(result[:], back[:, 0:width])
+            queue.dma_start(out[c * P : (c + 1) * P, h * HALF : h * HALF + width], result[:])
 
         def blend(c, into=None, first=whole):
             diffs = []
@@ -304,7 +306,9 @@ def tile_list_hwayt_mix_silu_kernel(
         first_sum = turned_sum(gated[2][0], silus[2][0], "bank_a")
         tanhs[3] = [gate_half(3, 0, "bank_f")]
         tanhs[3].append(gate_half(3, 1, "bank_e"))
+        second_sum = turned_sum(gated[2][1][:, quarters[0]], silus[2][1][:, quarters[0]], "bank_b", True)
         turn_back(2, 0, first_sum, "bank_d", nc.scalar)
+        turn_back(2, 1, second_sum, "bank_c", nc.scalar)
         c = CHUNKS - 1
         pieces = [slice(0, HALF), slice(HALF, HALF + HALF // 2), slice(HALF + HALF // 2, J)]
         diffs, blends = {}, {}
@@ -331,7 +335,11 @@ def tile_list_hwayt_mix_silu_kernel(
             nc.sync.dma_start(out[c * P : (c + 1) * P, js], result[:])
 
         last_diff(0)
-        direct_sum(2, [1])
+        rest = keep.tile([P, HALF // 2], F32, name="result2_rest")
+        nc.vector.scalar_tensor_tensor(
+            rest[:], gated[2][1][:, quarters[1]], 0.5, silus[2][1][:, quarters[1]], ALU.mult, ALU.add
+        )
+        nc.sync.dma_start(out[2 * P : 3 * P, HALF + HALF // 2 : J], rest[:])
         last_diff(1)
         last_blend(0)
         last_diff(2)

@@ -27,10 +27,10 @@ GROUP = 16
 QUADRANT = 32
 SCALE_ROWS = 4
 SECOND_ROWS = 16
-EARLY = 2
+PAIR = 2
+BIAS_STEP = 8
 RUN = 4
-TURNED = (1, 2)
-LAST_PIECES = 2
+HELD = 3
 
 
 def tile_list_hwayt_mix_silu_kernel(
@@ -57,8 +57,6 @@ def tile_list_hwayt_mix_silu_kernel(
         bias_rows = keep.tile([P, QUADRANT], F32, name="bias_rows", align_bytes=64)
         scaled_rows = keep.tile([P, QUADRANT], F32, name="scaled_rows", align_bytes=64)
         tanh_bias = keep.tile([P, QUADRANT], F32, name="tanh_bias", align_bytes=64)
-        identity = keep.tile([P, P], F32, name="identity")
-        make_identity(nc, identity[:])
 
         nc.vector.memset(scale_window[:], 0)
         nc.vector.memset(wg8_plane[:], 0)
@@ -76,15 +74,15 @@ def tile_list_hwayt_mix_silu_kernel(
 
         wh_rows = wh.rearrange("(a p i) n -> a p i n", a=PASSES, i=PACK)
         wh_raw = {}
-        early_bytes = PACK * EARLY * P * 4
+        early_bytes = PACK * PAIR * P * 4
 
         def load_wh(tile, first, a):
-            nc.sync.dma_start(tile, wh_rows[a][:, :, first * P : (first + EARLY) * P])
-            for k in range(EARLY):
+            nc.sync.dma_start(tile, wh_rows[a][:, :, first * P : (first + PAIR) * P])
+            for k in range(PAIR):
                 wh_raw[first + k, a] = tile[:, :, k * P : (k + 1) * P]
 
-        def load_carried(c, cols=slice(0, T)):
-            nc.sync.dma_start(carried[c][:, cols], rT[c * P : (c + 1) * P, cols])
+        def load_carried(c):
+            nc.sync.dma_start(carried[c][:, 0:T], rT[c * P : (c + 1) * P, 0:T])
 
         nc.sync.dma_start(offsets[:], offs)
         wg8_rows = wg8_words[0].rearrange("p n b -> p (n b)").bitcast(I32)
@@ -94,9 +92,9 @@ def tile_list_hwayt_mix_silu_kernel(
             nc.sync.dma_start(scale_window[r:P:SECOND_ROWS, :], table_rows[r])
         nc.sync.dma_start(word_window[:], tab_words[0].rearrange("p t b -> p (t b)").bitcast(I32))
         load_plane(wg8_plane, wg8_scales)
-        nc.sync.dma_start(bias_rows[0:P:8, :], bg.rearrange("(c b i) -> b c i", c=CHUNKS, b=P // QUADRANT))
+        nc.sync.dma_start(bias_rows[0:P:BIAS_STEP, :], bg.rearrange("(c b i) -> b c i", c=CHUNKS, b=P // QUADRANT))
         early_wh = [
-            reused.tile([P, PACK, EARLY * P], F32, name=f"early_wh{a}", offset=a * early_bytes, align_bytes=64)
+            reused.tile([P, PACK, PAIR * P], F32, name=f"early_wh{a}", offset=a * early_bytes, align_bytes=64)
             for a in range(PASSES)
         ]
         for a in range(PASSES):
@@ -112,13 +110,14 @@ def tile_list_hwayt_mix_silu_kernel(
         load_carried(0)
         load_plane(wg4_plane, wg4_scales)
         nc.sync.dma_start(wg4_codes[:], wg4_words[0].bitcast(I32))
-        late_first = keep.tile([P, PACK, EARLY * P], F32, name="late_first")
-        load_wh(late_first[:], EARLY, 0)
+        late_first = keep.tile([P, PACK, PAIR * P], F32, name="late_first")
+        load_wh(late_first[:], PAIR, 0)
         nc.sync.dma_start(wg8_codes[1][:], wg8_rows[:, N // 2 : N])
         load_carried(1)
         late_offset = PASSES * early_bytes
-        late_second = reused.tile([P, 6, EARLY * P], F32, name="late_second", offset=late_offset, align_bytes=64)
-        load_wh(late_second[:, 0:PACK, :], EARLY, 1)
+        late_rows = HELD * HALF // (PAIR * P)
+        late_second = reused.tile([P, late_rows, PAIR * P], F32, name="late_second", offset=late_offset, align_bytes=64)
+        load_wh(late_second[:, 0:PACK, :], PAIR, 1)
         load_carried(2)
         load_carried(3)
 
@@ -148,40 +147,42 @@ def tile_list_hwayt_mix_silu_kernel(
 
         each_pass = [slice(a, a + 1) for a in range(PASSES)]
         both_passes = [slice(0, PASSES)]
+        whole = [slice(0, HALF)]
+        quarters = [slice(0, HALF // 2), slice(HALF // 2, HALF)]
 
         item_codes = []
-
         picked_words = {}
-        picked_offset = late_offset + 6 * EARLY * P * 4
+        picked_offset = late_offset + HELD * HALF * 4
+
+        def listed(h, js):
+            return offsets[:, (h * HALF + js.start) // GROUP : (h * HALF + js.stop) // GROUP]
 
         def pick_words(h, js, place):
             picked = reused.tile(
                 [P, js.stop - js.start], I32, name=f"picked{h}_{js.start}", offset=place, align_bytes=64
             )
-            picks = offsets[:, (h * HALF + js.start) // GROUP : (h * HALF + js.stop) // GROUP]
-            nc.vector.tensor_copy(picked[:].bitcast(U32), word_window[:].bitcast(U32).indirect(picks))
+            nc.vector.tensor_copy(picked[:].bitcast(U32), word_window[:].bitcast(U32).indirect(listed(h, js)))
             picked_words[h, js.start] = picked
 
-        def part_words(h, parted, pieces):
-            for js in pieces:
+        def part_words(h, parted):
+            for js in quarters:
                 nc.vector.tensor_copy(
                     parted[:, :, js], picked_words[h, js.start][:].bitcast(U16).rearrange("p (j a) -> p a j", a=PASSES)
                 )
             item_codes.append(parted)
 
-        whole = [slice(0, HALF)]
-        quarters = [slice(0, HALF // 2), slice(HALF // 2, HALF)]
-
-        for c in range(EARLY):
+        for c in range(PAIR):
             round_wh(c)
         pick_words(0, quarters[0], picked_offset)
         pick_words(0, quarters[1], picked_offset + HALF * 2)
-        part_words(0, keep.tile([P, PASSES, HALF], U16, name="parted0", align_bytes=64), quarters)
+        part_words(0, keep.tile([P, PASSES, HALF], U16, name="parted0", align_bytes=64))
+        identity = reused.tile([P, P], F32, name="identity", offset=picked_offset + HALF * 2, align_bytes=64)
+        make_identity(nc, identity[:])
         pick_words(1, quarters[0], picked_offset)
         quantise_wh(0, each_pass[:1])
         pick_words(1, quarters[1], 0)
         quantise_wh(0, each_pass[1:])
-        part_words(1, reused.tile([P, PASSES, HALF], U16, name="parted1", offset=early_bytes, align_bytes=64), quarters)
+        part_words(1, reused.tile([P, PASSES, HALF], U16, name="parted1", offset=early_bytes, align_bytes=64))
         quantise_wh(1, both_passes)
         nc.scalar.mul(scaled_rows[:], bias_rows[:], -0.5)
         nc.vector.transpose(tanh_bias[:], scaled_rows[:])
@@ -210,15 +211,15 @@ def tile_list_hwayt_mix_silu_kernel(
 
         def gate_half(c, h, bank, order=(1, 0), tanh=None):
             cols = slice(c * P, (c + 1) * P)
-            own = slice(c % 2 * P, (c % 2 + 1) * P)
+            own = slice(c % PAIR * P, (c % PAIR + 1) * P)
             weights = [
-                (wg8_codes[c // 2][:, own].bitcast(FP8X4), wg8_plane[:].bitcast(U8)[:, cols]),
+                (wg8_codes[c // PAIR][:, own].bitcast(FP8X4), wg8_plane[:].bitcast(U8)[:, cols]),
                 (wg4_codes[:].bitcast(FP4X4)[:, cols], wg4_plane[:].bitcast(U8)[:, cols]),
             ]
             acc = product(bank, h, weights, order)
             if tanh is None:
                 tanh = keep.tile([P, HALF], F32, name=f"tanh{c}_{h}")
-            nc.scalar.activation(tanh[:], acc, ACT.Tanh, bias=tanh_bias[:, 8 * c : 8 * c + 1], scale=-0.5)
+            nc.scalar.activation(tanh[:], acc, ACT.Tanh, bias=tanh_bias[:, BIAS_STEP * c : BIAS_STEP * c + 1], scale=-0.5)
             return tanh
 
         def turned_sum(twice, silu, bank, blend_first=False):
@@ -255,8 +256,9 @@ def tile_list_hwayt_mix_silu_kernel(
             for h in range(HALVES):
                 diff = ring.tile([P, HALF], F32, name="diff")
                 for js in first if h == 0 else whole:
-                    picks = offsets[:, (h * HALF + js.start) // GROUP : (h * HALF + js.stop) // GROUP]
-                    nc.vector.tensor_tensor(diff[:, js], carried[c][:].indirect(picks), silus[c][h][:, js], ALU.subtract)
+                    nc.vector.tensor_tensor(
+                        diff[:, js], carried[c][:].indirect(listed(h, js)), silus[c][h][:, js], ALU.subtract
+                    )
                 diffs.append(diff)
             halves = []
             for h in range(HALVES):
@@ -265,16 +267,10 @@ def tile_list_hwayt_mix_silu_kernel(
                 halves.append(twice)
             return halves
 
-        def direct_sum(c, halves=range(HALVES)):
-            for h in halves:
-                pieces = LAST_PIECES if (c, h) == (CHUNKS - 1, HALVES - 1) else 1
-                width = HALF // pieces
-                for k in range(pieces):
-                    js = slice(k * width, (k + 1) * width)
-                    result = keep.tile([P, width], F32, name=f"result{c}_{h}_{k}")
-                    nc.vector.scalar_tensor_tensor(result[:], gated[c][h][:, js], 0.5, silus[c][h][:, js], ALU.mult, ALU.add)
-                    column = h * HALF + k * width
-                    nc.sync.dma_start(out[c * P : (c + 1) * P, column : column + width], result[:])
+        def direct_sum(c, h, js, name):
+            result = keep.tile([P, js.stop - js.start], F32, name=name)
+            nc.vector.scalar_tensor_tensor(result[:], gated[c][h][:, js], 0.5, silus[c][h][:, js], ALU.mult, ALU.add)
+            nc.sync.dma_start(out[c * P : (c + 1) * P, h * HALF + js.start : h * HALF + js.stop], result[:])
 
         def after_rounding(n, name):
             return reused.tile([P, HALF], F32, name=name, offset=late_offset + n * HALF * 4, align_bytes=64)
@@ -284,13 +280,14 @@ def tile_list_hwayt_mix_silu_kernel(
         tanhs = {0: [gate_half(0, 0, "bank_c", (0, 1)), gate_half(0, 1, "bank_h", (0, 1))]}
         silus[1].append(transform_half(1, 1, ["bank_c"]))
         gated = {0: blend(0, first=quarters)}
-        direct_sum(0)
-        for c in (2, 3):
+        for h in range(HALVES):
+            direct_sum(0, h, whole[0], f"result0_{h}_0")
+        for c in range(PAIR, CHUNKS):
             round_wh(c, [0])
             quantise_wh(c, each_pass[:1])
         tanhs[1] = [gate_half(1, 0, "bank_f", (0, 1)), gate_half(1, 1, "bank_c")]
         tanhs[2] = [gate_half(2, 0, "bank_e", (0, 1))]
-        for c in (2, 3):
+        for c in range(PAIR, CHUNKS):
             round_wh(c, [1])
             quantise_wh(c, each_pass[1:])
         tanhs[2].append(gate_half(2, 1, "bank_e", tanh=after_rounding(2, "tanh2_1")))
@@ -335,11 +332,7 @@ def tile_list_hwayt_mix_silu_kernel(
             nc.sync.dma_start(out[c * P : (c + 1) * P, js], result[:])
 
         last_diff(0)
-        rest = keep.tile([P, HALF // 2], F32, name="result2_rest")
-        nc.vector.scalar_tensor_tensor(
-            rest[:], gated[2][1][:, quarters[1]], 0.5, silus[2][1][:, quarters[1]], ALU.mult, ALU.add
-        )
-        nc.sync.dma_start(out[2 * P : 3 * P, HALF + HALF // 2 : J], rest[:])
+        direct_sum(2, 1, quarters[1], "result2_rest")
         last_diff(1)
         last_blend(0)
         last_diff(2)

from contextlib import ExitStack

import concourse.mybir as mybir
from concourse.masks import make_identity

K, N, T, J = 1024, 512, 2048, 1024
FLOPS = 2 * 2 * K * N * J

F32 = mybir.dt.float32
BF16 = mybir.dt.bfloat16
I32 = mybir.dt.int32
U32 = mybir.dt.uint32
U16 = mybir.dt.uint16
U8 = mybir.dt.uint8
FP8X4 = mybir.dt.float8_e4m3fn_x4
FP4X4 = mybir.dt.float4_e2m1fn_x4
ACT = mybir.ActivationFunctionType
ALU = mybir.AluOpType

P = 128
PACK = 4
PASSES = K // (P * PACK)
CHUNKS = N // P
HALF = 512
HALVES = J // HALF
GROUP = 16
QUADRANT = 32
SCALE_ROWS = 4
SECOND_ROWS = 16
PAIR = 2
BIAS_STEP = 8
RUN = 4
HELD = 3


def tile_list_hwayt_mix_silu_kernel(
    tc, tab_words, tab_scales, wg8_words, wg8_scales, wg4_words, wg4_scales, wh, bg, rT, offs, out
):
    nc = tc.nc
    with ExitStack() as ctx:
        keep = ctx.enter_context(tc.tile_pool(name="keep", bufs=1))
        ring = ctx.enter_context(tc.tile_pool(name="ring", bufs=6))
        reused = ctx.enter_context(tc.tile_pool(name="reused", bufs=1))
        psum = ctx.enter_context(tc.psum_pool(name="psum", bufs=1))

        offsets = keep.tile([P, J // GROUP], U16, name="offsets")
        scale_window = keep.tile([P, T // 4], I32, name="scale_window", align_bytes=64)
        word_window = keep.tile([P, T], I32, name="word_window", align_bytes=64)
        picked_scales = keep.tile([P, J], U8, name="picked_scales", align_bytes=64)
        second_plane = keep.tile([P, J // 4], I32, name="second_plane", align_bytes=64)
        item_planes = [picked_scales[:], second_plane[:].bitcast(U8)]
        wg8_codes = [keep.tile([P, N // 2], I32, name=f"wg8_codes{g}", align_bytes=64) for g in range(2)]
        wg4_codes = keep.tile([P, N // 2], I32, name="wg4_codes", align_bytes=64)
        wg8_plane = keep.tile([P, N // 4], I32, name="wg8_plane", align_bytes=64)
        wg4_plane = keep.tile([P, N // 4], I32, name="wg4_plane", align_bytes=64)
        carried = [keep.tile([P, T], F32, name=f"carried{c}", align_bytes=64) for c in range(CHUNKS)]
        bias_rows = keep.tile([P, QUADRANT], F32, name="bias_rows", align_bytes=64)
        scaled_rows = keep.tile([P, QUADRANT], F32, name="scaled_rows", align_bytes=64)
        tanh_bias = keep.tile([P, QUADRANT], F32, name="tanh_bias", align_bytes=64)

        nc.vector.memset(scale_window[:], 0)
        nc.vector.memset(wg8_plane[:], 0)
        nc.vector.memset(bias_rows[:], 0.0)
        nc.vector.memset(wg4_plane[:], 0)
        nc.vector.memset(second_plane[:], 0)

        warm = keep.tile([P, 1], F32, name="warm")
        nc.scalar.activation(warm[:], bias_rows[:, 0:1], ACT.Silu)

        def load_plane(plane, scales):
            rows = scales[0].bitcast(I32).rearrange("(q r) n -> r q n", r=SCALE_ROWS)
            for r in range(SCALE_ROWS):
                nc.sync.dma_start(plane[r:P:QUADRANT, :], rows[r])

        wh_rows = wh.rearrange("(a p i) n -> a p i n", a=PASSES, i=PACK)
        wh_raw = {}
        early_bytes = PACK * PAIR * P * 4

        def load_wh(tile, first, a):
            nc.sync.dma_start(tile, wh_rows[a][:, :, first * P : (first + PAIR) * P])
            for k in range(PAIR):
                wh_raw[first + k, a] = tile[:, :, k * P : (k + 1) * P]

        def load_carried(c):
            nc.sync.dma_start(carried[c][:, 0:T], rT[c * P : (c + 1) * P, 0:T])

        nc.sync.dma_start(offsets[:], offs)
        wg8_rows = wg8_words[0].rearrange("p n b -> p (n b)").bitcast(I32)
        nc.sync.dma_start(wg8_codes[0][:], wg8_rows[:, 0 : N // 2])
        table_rows = tab_scales.bitcast(I32).rearrange("a (q r) t -> r q a t", r=SCALE_ROWS)
        for r in range(SCALE_ROWS):
            nc.sync.dma_start(scale_window[r:P:SECOND_ROWS, :], table_rows[r])
        nc.sync.dma_start(word_window[:], tab_words[0].rearrange("p t b -> p (t b)").bitcast(I32))
        load_plane(wg8_plane, wg8_scales)
        nc.sync.dma_start(bias_rows[0:P:BIAS_STEP, :], bg.rearrange("(c b i) -> b c i", c=CHUNKS, b=P // QUADRANT))
        early_wh = [
            reused.tile([P, PACK, PAIR * P], F32, name=f"early_wh{a}", offset=a * early_bytes, align_bytes=64)
            for a in range(PASSES)
        ]
        for a in range(PASSES):
            load_wh(early_wh[a][:], 0, a)

        nc.vector.tensor_copy(picked_scales[:], scale_window[:].bitcast(U8).indirect(offsets[:]))
        for r in range(SCALE_ROWS):
            nc.sync.dma_start(
                second_plane[r:P:QUADRANT, :],
                picked_scales[:].bitcast(I32)[SECOND_ROWS + r : P : QUADRANT, :],
            )

        load_carried(0)
        load_plane(wg4_plane, wg4_scales)
        nc.sync.dma_start(wg4_codes[:], wg4_words[0].bitcast(I32))
        late_first = keep.tile([P, PACK, PAIR * P], F32, name="late_first")
        load_wh(late_first[:], PAIR, 0)
        nc.sync.dma_start(wg8_codes[1][:], wg8_rows[:, N // 2 : N])
        load_carried(1)
        late_offset = PASSES * early_bytes
        late_rows = HELD * HALF // (PAIR * P)
        late_second = reused.tile([P, late_rows, PAIR * P], F32, name="late_second", offset=late_offset, align_bytes=64)
        load_wh(late_second[:, 0:PACK, :], PAIR, 1)
        load_carried(2)
        load_carried(3)

        grouped = {}
        wh_codes = {}
        wh_plane = {}

        for c in range(CHUNKS):
            grouped[c] = keep.tile([P, PASSES, P, PACK], BF16, name=f"grouped{c}", align_bytes=64)
            wh_codes[c] = keep.tile([P, PASSES, P], U32, name=f"wh_codes{c}", align_bytes=64)
            wh_plane[c] = keep.tile([P, PASSES, P], U8, name=f"wh_plane{c}", align_bytes=64)

        def round_wh(c, passes=range(PASSES)):
            for a in passes:
                nc.scalar.copy(
                    grouped[c][:, a].rearrange("p (m v) i -> p m i v", v=RUN),
                    wh_raw[c, a].rearrange("p i (m v) -> p m i v", v=RUN),
                )

        def quantise_wh(c, calls):
            for passes in calls:
                nc.vector.quantize_mx(
                    out=wh_codes[c][:, passes].rearrange("p a n -> p (a n)").bitcast(FP8X4),
                    scales=wh_plane[c][:, passes].rearrange("p a n -> p (a n)"),
                    in_=grouped[c][:, passes].rearrange("p a n i -> p (a n i)"),
                )

        each_pass = [slice(a, a + 1) for a in range(PASSES)]
        both_passes = [slice(0, PASSES)]
        whole = [slice(0, HALF)]
        quarters = [slice(0, HALF // 2), slice(HALF // 2, HALF)]

        item_codes = []
        picked_words = {}
        picked_offset = late_offset + HELD * HALF * 4

        def listed(h, js):
            return offsets[:, (h * HALF + js.start) // GROUP : (h * HALF + js.stop) // GROUP]

        def pick_words(h, js, place):
            picked = reused.tile(
                [P, js.stop - js.start], I32, name=f"picked{h}_{js.start}", offset=place, align_bytes=64
            )
            nc.vector.tensor_copy(picked[:].bitcast(U32), word_window[:].bitcast(U32).indirect(listed(h, js)))
            picked_words[h, js.start] = picked

        def part_words(h, parted):
            for js in quarters:
                nc.vector.tensor_copy(
                    parted[:, :, js], picked_words[h, js.start][:].bitcast(U16).rearrange("p (j a) -> p a j", a=PASSES)
                )
            item_codes.append(parted)

        for c in range(PAIR):
            round_wh(c)
        pick_words(0, quarters[0], picked_offset)
        pick_words(0, quarters[1], picked_offset + HALF * 2)
        part_words(0, keep.tile([P, PASSES, HALF], U16, name="parted0", align_bytes=64))
        identity = reused.tile([P, P], F32, name="identity", offset=picked_offset + HALF * 2, align_bytes=64)
        make_identity(nc, identity[:])
        pick_words(1, quarters[0], picked_offset)
        quantise_wh(0, each_pass[:1])
        pick_words(1, quarters[1], 0)
        quantise_wh(0, each_pass[1:])
        part_words(1, reused.tile([P, PASSES, HALF], U16, name="parted1", offset=early_bytes, align_bytes=64))
        quantise_wh(1, both_passes)
        nc.scalar.mul(scaled_rows[:], bias_rows[:], -0.5)
        nc.vector.transpose(tanh_bias[:], scaled_rows[:])

        def product(bank, h, weights, order=(0, 1), js=slice(0, HALF)):
            acc = psum.tile([P, HALF], F32, name=bank)[:, 0 : js.stop - js.start]
            for a in order:
                codes, plane = weights[a]
                nc.tensor.matmul_mx(
                    out=acc,
                    lhsT=codes,
                    lhsT_scale=plane,
                    rhs=item_codes[h][:, a, js].bitcast(FP4X4),
                    rhs_scale=item_planes[a][:, h * HALF + js.start : h * HALF + js.stop],
                    start=(a == order[0]),
                    stop=(a == order[-1]),
                )
            return acc

        def transform_half(c, h, banks, order=(0, 1)):
            weights = [(wh_codes[c][:, a, :].bitcast(FP8X4), wh_plane[c][:, a, :]) for a in range(PASSES)]
            silu = keep.tile([P, HALF], F32, name=f"silu{c}_{h}")
            for bank, js in zip(banks, whole if len(banks) == 1 else quarters):
                nc.scalar.activation(silu[:, js], product(bank, h, weights, order, js), ACT.Silu)
            return silu

        def gate_half(c, h, bank, order=(1, 0), tanh=None):
            cols = slice(c * P, (c + 1) * P)
            own = slice(c % PAIR * P, (c % PAIR + 1) * P)
            weights = [
                (wg8_codes[c // PAIR][:, own].bitcast(FP8X4), wg8_plane[:].bitcast(U8)[:, cols]),
                (wg4_codes[:].bitcast(FP4X4)[:, cols], wg4_plane[:].bitcast(U8)[:, cols]),
            ]
            acc = product(bank, h, weights, order)
            if tanh is None:
                tanh = keep.tile([P, HALF], F32, name=f"tanh{c}_{h}")
            nc.scalar.activation(tanh[:], acc, ACT.Tanh, bias=tanh_bias[:, BIAS_STEP * c : BIAS_STEP * c + 1], scale=-0.5)
            return tanh

        def turned_sum(twice, silu, bank, blend_first=False):
            total = psum.tile([P, HALF], F32, name=bank)
            width = twice.shape[1]
            terms = [twice, silu, silu] if blend_first else [silu, silu, twice]
            for n, term in enumerate(terms):
                for b in range(width // P):
                    cols = slice(b * P, (b + 1) * P)
                    nc.tensor.matmul(
                        total[:, cols],
                        lhsT=term[:, cols],
                        rhs=identity[:],
                        is_transpose=True,
                        start=(n == 0 and b == 0),
                        stop=(n == len(terms) - 1 and b == width // P - 1),
                    )
            halved = ring.tile([P, HALF], F32, name="halved")
            nc.scalar.mul(halved[:, 0:width], total[:, 0:width], 0.5)
            return halved[:, 0:width]

        def turn_back(c, h, halved, bank, queue=nc.sync):
            width = halved.shape[1]
            back = psum.tile([P, HALF], F32, name=bank)
            for b in range(width // P):
                cols = slice(b * P, (b + 1) * P)
                nc.tensor.transpose(back[:, cols], halved[:, cols], identity[:])
            result = keep.tile([P, width], F32, name=f"result{c}_{h}")
            nc.scalar.copy(result[:], back[:, 0:width])
            queue.dma_start(out[c * P : (c + 1) * P, h * HALF : h * HALF + width], result[:])

        def blend(c, into=None, first=whole):
            diffs = []
            for h in range(HALVES):
                diff = ring.tile([P, HALF], F32, name="diff")
                for js in first if h == 0 else whole:
                    nc.vector.tensor_tensor(
                        diff[:, js], carried[c][:].indirect(listed(h, js)), silus[c][h][:, js], ALU.subtract
                    )
                diffs.append(diff)
            halves = []
            for h in range(HALVES):
                twice = ring.tile([P, HALF], F32, name="twice") if into is None else into[h]
                nc.vector.scalar_tensor_tensor(twice[:], tanhs[c][h][:], 1.0, diffs[h][:], ALU.add, ALU.mult)
                halves.append(twice)
            return halves

        def direct_sum(c, h, js, name):
            result = keep.tile([P, js.stop - js.start], F32, name=name)
            nc.vector.scalar_tensor_tensor(result[:], gated[c][h][:, js], 0.5, silus[c][h][:, js], ALU.mult, ALU.add)
            nc.sync.dma_start(out[c * P : (c + 1) * P, h * HALF + js.start : h * HALF + js.stop], result[:])

        def after_rounding(n, name):
            return reused.tile([P, HALF], F32, name=name, offset=late_offset + n * HALF * 4, align_bytes=64)

        silus = {0: [transform_half(0, 0, ["bank_h", "bank_a"]), transform_half(0, 1, ["bank_b"], (1, 0))]}
        silus[1] = [transform_half(1, 0, ["bank_a"])]
        tanhs = {0: [gate_half(0, 0, "bank_c", (0, 1)), gate_half(0, 1, "bank_h", (0, 1))]}
        silus[1].append(transform_half(1, 1, ["bank_c"]))
        gated = {0: blend(0, first=quarters)}
        for h in range(HALVES):
            direct_sum(0, h, whole[0], f"result0_{h}_0")
        for c in range(PAIR, CHUNKS):
            round_wh(c, [0])
            quantise_wh(c, each_pass[:1])
        tanhs[1] = [gate_half(1, 0, "bank_f", (0, 1)), gate_half(1, 1, "bank_c")]
        tanhs[2] = [gate_half(2, 0, "bank_e", (0, 1))]
        for c in range(PAIR, CHUNKS):
            round_wh(c, [1])
            quantise_wh(c, each_pass[1:])
        tanhs[2].append(gate_half(2, 1, "bank_e", tanh=after_rounding(2, "tanh2_1")))
        silus[2] = [transform_half(2, 0, ["bank_a", "bank_g"]), transform_half(2, 1, ["bank_b"])]
        gated[1] = blend(1, [after_rounding(h, f"twice1_{h}") for h in range(HALVES)])
        first_sum = turned_sum(gated[1][0], silus[1][0], "bank_h")
        silus[3] = [transform_half(3, 0, ["bank_e"])]
        second_sum = turned_sum(gated[1][1], silus[1][1], "bank_c")
        turn_back(1, 0, first_sum, "bank_f")
        silus[3].append(transform_half(3, 1, ["bank_e"]))
        turn_back(1, 1, second_sum, "bank_g")
        gated[2] = blend(2, first=quarters)
        first_sum = turned_sum(gated[2][0], silus[2][0], "bank_a")
        tanhs[3] = [gate_half(3, 0, "bank_f")]
        tanhs[3].append(gate_half(3, 1, "bank_e"))
        second_sum = turned_sum(gated[2][1][:, quarters[0]], silus[2][1][:, quarters[0]], "bank_b", True)
        turn_back(2, 0, first_sum, "bank_d", nc.scalar)
        turn_back(2, 1, second_sum, "bank_c", nc.scalar)
        c = CHUNKS - 1
        pieces = [slice(0, HALF), slice(HALF, HALF + HALF // 2), slice(HALF + HALF // 2, J)]
        diffs, blends = {}, {}

        def of_piece(halves, js):
            h = js.start // HALF
            return halves[h][:, js.start - h * HALF : js.stop - h * HALF]

        def last_diff(n):
            js = pieces[n]
            diffs[n] = keep.tile([P, js.stop - js.start], F32, name=f"last_diff{n}")
            picks = offsets[:, js.start // GROUP : js.stop // GROUP]
            nc.vector.tensor_tensor(diffs[n][:], carried[c][:].indirect(picks), of_piece(silus[c], js), ALU.subtract)

        def last_blend(n):
            js = pieces[n]
            blends[n] = keep.tile([P, js.stop - js.start], F32, name=f"last_blend{n}")
            nc.vector.scalar_tensor_tensor(blends[n][:], of_piece(tanhs[c], js), 1.0, diffs[n][:], ALU.add, ALU.mult)

        def last_sum(n):
            js = pieces[n]
            result = keep.tile([P, js.stop - js.start], F32, name=f"last_result{n}")
            nc.vector.scalar_tensor_tensor(result[:], blends[n][:], 0.5, of_piece(silus[c], js), ALU.mult, ALU.add)
            nc.sync.dma_start(out[c * P : (c + 1) * P, js], result[:])

        last_diff(0)
        direct_sum(2, 1, quarters[1], "result2_rest")
        last_diff(1)
        last_blend(0)
        last_diff(2)
        last_sum(0)
        last_blend(1)
        last_blend(2)
        last_sum(1)
        last_sum(2)
